import numpy as np, ml_dtypes
CORES = [6,15,38,47]
N = 4
BF = ml_dtypes.bfloat16
V, M, S, CAP, P, RO, STEP, LN = 2048, 4096, 256, 64, 8, 3, 650, 2
W1 = 13 * np.arange(16) + 5; W2 = 255 - 14 * np.arange(16); A = N * CAP
def mix(d):
    u = np.add.reduce(W1[:, None] * d, axis=2) & 4095; w = np.add.reduce(W2[:, None] * d, axis=2) & 4095
    return u, (u * w) >> 5
def kid(d, c, hm, t):
    R, n = d.shape[0], d.shape[3]
    hv = np.take_along_axis(hm, d.reshape(R, 8, 1, 16 * n), 3).reshape(R, 8, 16, 16, n)
    e = np.add.reduce(np.minimum(hv, np.abs(c)[:, :, :, None]), axis=2)
    k = np.argmax(e, axis=2); u, h = mix(d); v = (h + 37 * np.max(e, axis=2) + t) & 4095
    void = np.any(d == v[:, :, None], axis=2) | (v >= M)
    new = np.where(np.arange(16)[:, None] == k[:, :, None], v[:, :, None], d)
    q = np.add.reduce((new < v[:, :, None]).astype(np.int64), axis=2)
    return ~void, np.sort(new, axis=2), np.where((((q - k) & 1) == 1)[:, :, None], -(c >> 2), c >> 2)
def spawn(D, C, hm, t):
    start = STEP * (t + 1); a = np.roll(np.any(C != 0, axis=2), -start, axis=2)
    o = np.argsort(~a, axis=2, kind="stable")[:, :, :S]; on = np.take_along_axis(a, o, 2); pl = (o + start) & (V - 1)
    good, ch, c = kid(np.take_along_axis(D, pl[:, :, None], 3), np.take_along_axis(C, pl[:, :, None], 3), hm, t)
    return pl, on, on & good, ch, c
def recs(rng, shape):
    return np.sort(rng.integers(0, M - 15, shape), axis=-2) + np.arange(16)[:, None]
def base(rng, share=None):
    lim = rng.choice(np.array([1, 3, 20, 127]), (N, 8, 1, V), p=[0.15, 0.15, 0.2, 0.5]); C = rng.integers(-lim, lim + 1, (N, 8, 16, V))
    if share is None: share = rng.choice(np.array([0.4, 0.55, 0.75, 0.92]), (N, 8, 1, 1))
    C = C * (rng.random((N, 8, 1, V)) < share)
    return recs(rng, (N, 8, 16, V)), C, rng.integers(0, 128, (N, 8, 16, M))
def plant(rng, D, C, hm, part, twin=False, t=0, own=False):
    live = np.any(C != 0, axis=2); pl, on, good, ch, c = spawn(D, C, hm, t); u, h = mix(ch)
    busy = np.zeros((N, 8, V), bool); np.put_along_axis(busy, pl, on, 2)
    q, g, s = np.nonzero(good & (rng.random(good.shape) < part)); r = h[q, g, s] & (N - 1)
    p = ((h[q, g, s] >> LN) + rng.integers(0, P, q.size) * (2 * u[q, g, s] + 1)) & (V - 1)
    one = np.unique((r * 8 + g) * V + p, return_index=True)[1]
    if not own: one = one[~busy[r[one], g[one], p[one]]]
    q, g, s, r, p = q[one], g[one], s[one], r[one], p[one]
    rec = ch[q, g, :, s]; w = c[q, g, :, s]; lv = live[r, g, p][:, None]; bs = busy[r, g, p][:, None]; n = one.size
    if twin:
        nxt = np.concatenate([rec[:, 1:], np.full((n, 1), M)], axis=1); way = rng.random(n)
        fit = (rec[:, :14] + 1 < rec[:, 1:15] - 2) & (rec[:, 2:] + 1 < nxt[:, 2:]); i = np.argmax(fit * (0.01 + rng.random(fit.shape)), axis=1)
        z = np.nonzero(np.any(fit, axis=1) & (way < 0.4))[0]
        rec[z, i[z]] += 1; rec[z, i[z] + 1] -= 2; rec[z, i[z] + 2] += 1
        i = np.where(rng.random(n) < 0.3, 15, rng.integers(0, 16, n))
        z = np.nonzero((way > 0.6) & (rec[np.arange(n), i] + 1 < nxt[np.arange(n), i]))[0]
        rec[z, i[z]] += 1
    D[r, g, :, p] = rec
    mode = rng.integers(0, 4, (n, 1)); old = C[r, g, :, p]; some = np.any(w != 0, axis=1)[:, None]
    new = np.where(lv & (mode == 0) & some, -w, np.where(lv & (mode == 1), np.where(w < 0, -127, 127), old))
    C[r, g, :, p] = np.where(bs & (mode == 3), rng.choice(np.array([-1, 1]), (n, 16)), new)
def pack(D, C, hm):
    return {"det": np.ascontiguousarray((256 * D + C + 128).reshape(N, 128, V)).astype(np.int32), "ham": np.ascontiguousarray(hm.reshape(N, 128, M)).astype(np.float32).astype(BF)}
def setup_inputs(rng):
    D, C, hm = base(rng)
    for t in range(RO - 1, -1, -1): plant(rng, D, C, hm, 0.35, False, t, True)
    return pack(D, C, hm)
def setup_inputs_slots(rng):
    D, C, hm = base(rng, 2.0); C[:, :, 0] = np.where(np.any(C != 0, axis=2), C[:, :, 0], 1)
    for q in range(N):
        good, ch, c = kid(D[q:q + 1], C[q:q + 1], hm[q:q + 1], 0); mine = good[0] & ((mix(ch)[1][0] & (N - 1)) == ((q + 1) & (N - 1)))
        for g in range(8):
            hit = rng.permutation(np.nonzero(mine[g])[0]); rest = rng.permutation(np.nonzero(~mine[g])[0])
            n = min((CAP, CAP + 1, CAP - 1, S, 0, 1, CAP, CAP + 1)[g], len(hit))
            seq = np.concatenate([rng.permutation(np.concatenate([hit[:n], rest[:S - n]])), rng.permutation(np.concatenate([hit[n:], rest[S - n:]]))])
            k = int(rng.integers(S, V - 63)); o = rng.permutation(V); at = (np.concatenate([np.sort(o[:k]), o[k:]]) + STEP) & (V - 1)
            d2 = np.zeros_like(D[q, g]); c2 = np.zeros_like(C[q, g])
            d2[:, at] = D[q, g][:, seq]; c2[:, at[:k]] = C[q, g][:, seq[:k]]; D[q, g] = d2; C[q, g] = c2
    return pack(D, C, hm)
def setup_inputs_ties(rng):
    D, C, hm = base(rng); ev = np.ascontiguousarray(D[:, ::2]); u, h = mix(ev)
    x = np.take_along_axis(ev, rng.integers(0, 16, (N, 4, 1, V)), 2); y = np.take_along_axis(ev, rng.integers(0, 16, (N, 4, 1, V)), 2)
    goal = rng.permuted(np.concatenate([x, x + 1, x - 1, y, y + 1, ev[:, :, :1], ev[:, :, 15:], 0 * x, 0 * x + M - 1, 0 * x + 4095], axis=2), axis=2)
    e = ((goal - h[:, :, None]) * pow(37, -1, 4096)) & 4095; ok = (e >= 1) & (e <= 2032)
    e = np.take_along_axis(e, np.argmax(ok, axis=2)[:, :, None], 2); ok = np.any(ok, axis=2)[:, :, None]
    z = (np.arange(16)[:, None] + rng.integers(0, 16, (N, 4, 1, V))) & 15
    new = ((e >> 4) + (z < (e & 15))) * rng.choice(np.array([-1, 1]), (N, 4, 16, V)); live = np.any(C[:, ::2] != 0, axis=2)[:, :, None]
    C[:, ::2] = np.where(ok & live, new, C[:, ::2])
    hm[:, ::2] = 127; hm[:, 1::2] = rng.choice(np.array([0, 9, 60]), (N, 4, 1, M))
    hm[np.arange(N), 2 * rng.integers(0, 4, N) + 1] = 0
    plant(rng, D, C, hm, 0.2)
    return pack(D, C, hm)
def setup_inputs_twins(rng):
    D, C, hm = base(rng); hm = np.repeat(hm[:1], N, axis=0); ix = rng.integers(0, 40, (N, 8, 1, V))
    pd = np.repeat(recs(rng, (1, 8, 16, 40)), N, axis=0)
    pc = np.repeat(np.where(np.arange(40) < 12, rng.integers(0, 4, (1, 8, 16, 40)), rng.integers(4, 128, (1, 8, 16, 40))), N, axis=0)
    use = rng.random((N, 8, 1, V)) < 0.6; live = np.any(C != 0, axis=2)[:, :, None]
    sign = np.where(rng.random((N, 8, 1, V)) < 0.4, 1, rng.choice(np.array([-1, 1]), (N, 8, 16, V)))
    D = np.where(use, np.take_along_axis(pd, ix, 3), D)
    C = np.where(use & live, np.take_along_axis(pc, ix, 3) * sign, C)
    plant(rng, D, C, hm, 0.5); plant(rng, D, C, hm, 0.4); plant(rng, D, C, hm, 0.4, True)
    return pack(D, C, hm)
def setup_inputs_thin(rng):
    D, C, hm = base(rng, 2.0); lone = np.arange(16)[:, None] == rng.integers(0, 16, (N, 8, 1, V))
    C[:, 1::2] = np.where(lone, np.where(C == 0, -1, C), 0)[:, 1::2]
    C[:, :, 0] = np.where(np.any(C != 0, axis=2), C[:, :, 0], 1); sizes = np.array([0, 1, 5, S - 1, S, S + 1, V - 1, V])
    for q in range(N):
        for g in range(8):
            n = int(sizes[g]) if q == 0 else int(rng.choice(sizes)); o = rng.permutation(V)
            if n == 5: o = np.array([0, V - 1, STEP - 1, STEP, STEP + 1])
            keep = np.zeros(V, np.int64); keep[o[:n]] = 1; C[q, g] = C[q, g] * keep
    plant(rng, D, C, hm, 0.3)
    return pack(D, C, hm)
def setup_inputs_spread(rng):
    D, C, hm = base(rng)
    D = np.sort(((M - 15) * rng.random((N, 8, 16, V)) ** rng.choice(np.array([1.0, 4.0]), (N, 8, 1, V))).astype(np.int64), axis=2) + np.arange(16)[:, None]
    size = np.exp2(7 * rng.random((N, 8, 1, V))); live = np.any(C != 0, axis=2)[:, :, None]
    C = np.minimum((size * rng.random((N, 8, 16, V))).astype(np.int64), 127) * rng.choice(np.array([-1, 1]), (N, 8, 16, V)) * live
    hm = np.minimum((np.exp2(7 * rng.random((N, 8, 1, M))) * rng.random((N, 8, 16, M))).astype(np.int64), 127)
    plant(rng, D, C, hm, 0.3)
    return pack(D, C, hm)
def check_inputs(d):
    bad = []
    x = d["det"].astype(np.int64).reshape(N, 8, 16, V); o = x >> 8
    if np.min(o) < 0 or np.max(o) > M - 1: bad.append("orbitals of det")
    if np.min(x & 255) < 1: bad.append("counts of det")
    if not np.all(o[:, :, 1:] > o[:, :, :-1]): bad.append("rising orbitals of det")
    h = d["ham"].astype(np.float32)
    if not np.all((h >= 0) & (h <= 127) & (h == np.floor(h))): bad.append("numbers of ham")
    return bad
def reference(det, ham):
    x = det.astype(np.int64).reshape(N, 8, 16, V); D = x >> 8; C = (x & 255) - 128
    hm = ham.astype(np.float32).astype(np.int64).reshape(N, 8, 16, M); num = np.arange(P)[:, None]
    for t in range(RO):
        pl, on, good, ch, c = spawn(D, C, hm, t)
        sel = np.zeros((N, 8, V), bool); np.put_along_axis(sel, pl, on, 2)
        C = C - np.sign(C) * sel[:, :, None]
        f = good[:, :, None] & ((mix(ch)[1] & (N - 1))[:, :, None] == np.arange(N)[:, None])
        before = np.add.accumulate(f.astype(np.int64), axis=3) - f.astype(np.int64)
        q, g, r, s = np.nonzero(f & (before < CAP)); a = q * CAP + before[q, g, r, s]
        ad = np.zeros((N, 8, 16, A), np.int64); ac = np.zeros((N, 8, 16, A), np.int64); there = np.zeros((N, 8, A), bool)
        ad[r, g, :, a] = ch[q, g, :, s]; ac[r, g, :, a] = c[q, g, :, s]; there[r, g, a] = True
        u, h = mix(ad)
        p = ((h >> LN)[:, :, None] + num * (2 * u + 1)[:, :, None]) & (V - 1)
        live = np.any(C != 0, axis=2); lp = np.take_along_axis(live, p.reshape(N, 8, P * A), 2).reshape(N, 8, P, A)
        dp = np.take_along_axis(D, p.reshape(N, 8, 1, P * A), 3).reshape(N, 8, 16, P, A)
        same = np.all(dp == ad[:, :, :, None], axis=2) & lp
        score = np.where(same, num, np.where(lp, 2 * P, P + num))
        ok = there & (np.min(score, axis=2) < 2 * P); place = np.take_along_axis(p, np.argmin(score, axis=2)[:, :, None], 2)[:, :, 0]
        r, g, a = np.nonzero(ok); low = np.full((N, 8, V), A); np.minimum.at(low, (r, g, place[r, g, a]), a)
        r, g, a = np.nonzero(ok & (np.take_along_axis(low, place, 2) == np.arange(A))); b = place[r, g, a]
        D[r, g, :, b] = ad[r, g, :, a]; C[r, g, :, b] = np.clip(C[r, g, :, b] + ac[r, g, :, a], -127, 127)
    return {"y": (256 * D + C + 128).reshape(N, 128, V).astype(np.float32)}

@@ -1,0 +1,568 @@
+from concourse.bass import DstId, RemoteDMATransfer
+from concourse.mybir import AluOpType as O, ActivationFunctionType as F
+
+RO, STEP, N, CAP = 3, 650, 4, 64
+TW = 2576
+DUMMY, DUMP = 2064, 2320
+K = 1 << 22
+F32, B16, H16, I32, U16 = "float32", "bfloat16", "float16", "int32", "uint16"
+
+WIDE = {
+    "detb": (2048, I32), "big": (2048, I32), "tab": (TW, F32), "cab": (TW, B16), "hamb": (4096, B16), "ones": (2048, B16),
+    "em": (2048, B16), "ep": (2048, B16), "e1": (2048, H16), "e2": (2048, H16), "bcb": (2048, B16), "bc": (2048, H16),
+    "rexp": (2048, B16), "lb0": (1024, B16), "lb1": (1024, B16), "lb2": (1024, B16), "rvkb": (512, B16), "rvk": (512, H16),
+    "mi": (1024, H16), "cmp": (2048, B16), "lg": (4096, B16), "mn": (4096, B16), "sb0": (1280, I32), "sb1": (1280, I32),
+    "sb2": (1280, I32), "ar0": (256, I32), "ar1": (256, I32), "ar2": (256, I32), "df": (2048, F32), "ab": (2048, F32),
+    "rl": (2048, B16), "eq": (4096, B16),
+}
+SMALL = {
+    F32: "pcol 1 cols 16 rr0 128 rr1 128 rr2 128 cw0 8 cw1 8 cw2 8 kscan 256 m80 80 sel15 128 iow 16 iow1 16 xio 256 mc 128 "
+         "dumpc 16 cneg 8 totu 1 bad4 16 cc 256 sgc 256 ff 256 km 256 ma 256 mb 256 lo 256 t1 256 tt 256 own2 16 inc 80 rk 80 "
+         "q2 256 cq 256 chp 256 pk 256 fs 256 fg 256 ft 256 aa 256 aam 256 k1 128 k2 128 k3 128 k4 64 k5 32 inv 16 keyw 16 "
+         "cs 256 cn 256 tg 256 tn 256 es 256 ls 16 ls2 16 fo 16",
+    B16: "blk 128 blk592 8 idb 128 shu 128 shd 128 cor 128 tmpb 128 mid 128 gum 128 gdm 128 ns0 128 ns1 128 ns2 128 ni0 128 "
+         "ni1 128 ni2 128 t10 128 t11 128 t12 128 t20 128 t21 128 t22 128 r00 256 r01 256 r02 256 negb 256 io0 256 io1 256 "
+         "a1 128 m128 128 trb 128 orow 80 zb 256 live 128 w 128 wz 128 val 256 abc 256 ct 256 sd 256 st_ 256 oh 80 fa 256 "
+         "ent 256 dm 256 lsb 256",
+    H16: "id16 128 gu16 128 gd16 128 w12 16 tm 256 nx 16 nt 16 d16 256 vk16 32 t32 128 ch16 256 mk 80 a16 256 hu 32 key16 16 kb16 256",
+    I32: "icol 1 icol2 1 ti 256 di 256 ci 256 fi 256 ui 32 ui2 32 pi 16 h16 16 h16t 16 si 16 vk 32 vo 16 vo2 16 own 16 npi 256 "
+         "npa 256 ai 256 ac 256 hi_ 16 sti 16 zi 128 zi2 128 kmi 16 m7 16 ms 16 msz 16 plc 16 oi 256 oc 256",
+    U16: "pl 16 du 256 sl 16 zu 128 plu 16 fou 16",
+}
+
+
+def _layout():
+    scratch, place = {}, {}
+    for i in range(8):
+        scratch["p%d" % i] = ("psum", [128, 512], F32)
+        place["p%d" % i] = ("p%d" % i, 0, 512)
+    for name in WIDE:
+        scratch[name] = ("sbuf", [128, WIDE[name][0]], WIDE[name][1])
+        place[name] = (name, 0, WIDE[name][0])
+    for dtype in SMALL:
+        words = SMALL[dtype].split()
+        at = 0
+        for j in range(0, len(words), 2):
+            w = int(words[j + 1])
+            place[words[j]] = ("w_" + dtype, at, w)
+            at += (w + 15) // 16 * 16
+        scratch["w_" + dtype] = ("sbuf", [128, at], dtype)
+    return scratch, place
+
+
+SCRATCH, PLACE = _layout()
+SEMAPHORES = ["sv", "ss", "st", "sg", "sent", "ldh"] + ["ld%d" % i for i in range(4)] + ["out%d" % i for i in range(4)] + ["arr%d" % i for i in range(RO)]
+SEMOF = {"v": "sv", "s": "ss", "t": "st", "g": "sg"}
+
+
+def plan(topo, cores, rank):
+    a = topo.chip(cores[rank])
+
+    def far(o):
+        b = topo.chip(cores[o])
+        return 0 if topo.mates(a, b) or topo.same_plane(a, b) else 1
+    out, used = [], 0
+    others = sorted([o for o in range(N) if o != rank], key=far)
+    for o in others:
+        n = 4 if o == others[-1] else 2
+        out.append((o, topo.engines(cores[rank], cores[o])[used:used + n]))
+        used += n
+    return out
+
+
+def rank_program(g, core, T, topo):
+    rank = T.rank_of(core)
+    if rank is None:
+        return
+    queues = {"v": g.vector, "s": g.scalar, "t": g.tensor, "g": g, "y": g.sync}
+    count = {"v": 0, "s": 0, "t": 0, "g": 0}
+    known = {q: {} for q in queues}
+    clock, hist, srcq = {}, {}, {}
+
+    def A(name, c0=0, c1=None, step=1, p0=0, p1=128):
+        buf, base, w = PLACE[name]
+        lo, hi = base + c0, base + (w if c1 is None else c1)
+        t = T[buf]
+        ap = t[p0:p1, lo:hi] if step == 1 else t[p0:p1, lo:hi:step]
+        return (ap, buf, lo, hi)
+
+    def P(b, c0, c1, step=1, p0=0, p1=128):
+        return A("p%d" % b, c0, c1, step, p0, p1)
+
+    def ind(win, off):
+        return (win[0].indirect(off[0]), win, off)
+
+    def flat(x):
+        return [x[1], x[2]] if len(x) == 3 else [x]
+
+    def ispsum(buf):
+        return buf[0] == "p" and buf[1:].isdigit()
+
+    def need(q, outs, ins, extra=()):
+        want = dict(extra)
+        acc = [(a, "w") for o in outs for a in flat(o)] + [(a, "r") for i in ins for a in flat(i)]
+        for (_, buf, lo, hi), kind in acc:
+            ps = ispsum(buf)
+            for (sq, idx, k2, l2, h2) in hist.get(buf, ()):
+                if sq == q == "t":
+                    continue
+                if (ps and sq != q) or ((kind == "w" or k2 == "w") and lo < h2 and l2 < hi):
+                    want[sq] = max(want.get(sq, 0), idx)
+        for s in sorted(want):
+            if known[q].get(s, 0) < want[s]:
+                queues[q].wait_ge(T.sem[SEMOF.get(s, s)], want[s])
+                known[q][s] = want[s]
+                for k, v in clock.get((s, want[s]), {}).items():
+                    known[q][k] = max(known[q].get(k, 0), v)
+        return acc
+
+    def note(q, idx, acc):
+        clock[(q, idx)] = dict(known[srcq.get(q, q)])
+        for (_, buf, lo, hi), kind in acc:
+            old = hist.get(buf, [])
+            if ispsum(buf):
+                keep = [e for e in old if e[0] == q and q != "t" and not (kind == "w" and lo <= e[3] and e[4] <= hi)]
+            else:
+                keep = [e for e in old if not (lo <= e[3] and e[4] <= hi and (kind == "w" or (e[2] == "r" and e[0] == q)))]
+            hist[buf] = keep + [(q, idx, kind, lo, hi)]
+
+    def emit(q, outs, ins, call, extra=()):
+        acc = need(q, outs, ins, extra)
+        r = call()
+        count[q] += 1
+        r.then_inc(T.sem[SEMOF[q]], 1)
+        note(q, count[q], acc)
+
+    def load(q, sem, out, src):
+        acc = need(q, [out], [])
+        queues[q].dma_start(out[0], src).then_inc(T.sem[sem], 16)
+        srcq[sem] = q
+        note(sem, 16, acc)
+
+    def store(q, sem, dst, i):
+        acc = need(q, [], [i])
+        queues[q].dma_start(dst, i[0]).then_inc(T.sem[sem], 16)
+        srcq[sem] = q
+        note(sem, 16, acc)
+
+    def mm(out, l, r, start=True, stop=True):
+        emit("t", [out], [l, r], lambda: g.tensor.matmul(out[0], l[0], r[0], start, stop))
+
+    def cp(out, i):
+        emit("v", [out], [i], lambda: g.vector.tensor_copy(out[0], i[0]))
+
+    def tt(out, a, b, op):
+        emit("v", [out], [a, b], lambda: g.vector.tensor_tensor(out[0], a[0], b[0], op))
+
+    def ts(out, i, s1, op0, s2=None, op1=None, extra=()):
+        ins = [i] + [s for s in (s1, s2) if isinstance(s, tuple)]
+        x1 = s1[0] if isinstance(s1, tuple) else s1
+        x2 = s2[0] if isinstance(s2, tuple) else s2
+        if op1 is None:
+            emit("v", [out], ins, lambda: g.vector.tensor_scalar(out[0], i[0], x1, None, op0), extra)
+        else:
+            emit("v", [out], ins, lambda: g.vector.tensor_scalar(out[0], i[0], x1, x2, op0, op1), extra)
+
+    def scan(out, a, b, op0, op1):
+        emit("v", [out], [a, b], lambda: g.vector.tensor_tensor_scan(out[0], a[0], b[0], 0.0, op0, op1))
+
+    def fill(out, c):
+        emit("v", [out], [], lambda: g.vector.memset(out[0], c))
+
+    def act(out, i, func, bias=0.0, scale=1.0):
+        ins = [i] + [s for s in (bias, scale) if isinstance(s, tuple)]
+        b = bias[0] if isinstance(bias, tuple) else bias
+        c = scale[0] if isinstance(scale, tuple) else scale
+        if func == F.Copy:
+            emit("s", [out], ins, lambda: g.scalar.activation(out[0], i[0], func))
+        else:
+            emit("s", [out], ins, lambda: g.scalar.activation(out[0], i[0], func, bias=b, scale=c))
+
+    def iota(out, pat, base, cm):
+        emit("g", [out], [], lambda: g.iota(out[0], pat, base, cm, allow_small_or_imprecise_dtypes=True))
+
+    def sel(out, i, pat, op, fillv, base, cm):
+        emit("g", [out], [i], lambda: g.affine_select(out[0], i[0], pat, op, fillv, base, cm))
+
+    one = lambda w: A("ones", 0, w)
+    col = lambda j: A("cols", j, j + 1)
+
+    for c in range(4):
+        load("y", "ld%d" % c, A("detb", 512 * c, 512 * c + 512), T.det[:, 512 * c:512 * c + 512])
+    load("s", "ldh", A("hamb"), T.ham[:, :])
+
+    fill(A("ones"), 1.0)
+    iota(A("icol"), [[0, 1]], 0, 1)
+    sel(A("tmpb"), one(128), [[-16, 8], [0, 16]], O.is_ge, 0.0, 0, 1)
+    sel(A("blk"), A("tmpb"), [[16, 8], [0, 16]], O.is_ge, 0.0, 15, -1)
+    ts(A("icol2"), A("icol"), 15, O.bitwise_and)
+    cp(A("pcol"), A("icol"))
+    cp(col(0), A("icol2"))
+    ts(col(1), col(0), 15.0, O.is_equal)
+    ts(col(2), col(1), 15.0, O.mult, 1.0, O.add)
+    ts(col(3), col(1), -1000.0, O.mult)
+    ts(col(4), col(1), 999.0, O.mult, 1.0, O.add)
+    ts(col(5), col(0), 13.0, O.mult, 5.0, O.add)
+    ts(col(6), col(0), -14.0, O.mult, 255.0, O.add)
+    ts(col(7), col(0), -1.0, O.mult, -2033.0, O.add)
+    ts(col(8), col(7), 8192.0, O.mult, 8192.0, O.add)
+    ts(col(9), col(1), -8192.0, O.mult)
+    ts(col(10), col(0), 0.0, O.is_equal, 8192.0, O.mult)
+    fill(A("zb"), 0.0)
+    fill(A("negb"), -1.0)
+    sel(A("idb"), one(128), [[-1, 128]], O.is_equal, 0.0, 0, 1)
+    sel(A("shu"), one(128), [[-1, 128]], O.is_equal, 0.0, -1, 1)
+    sel(A("cor"), one(128), [[-1, 128]], O.is_equal, 0.0, 127, 1)
+    sel(A("m128"), one(128), [[0, 8], [1, 16]], O.not_equal, 0.0, 0, 0)
+    sel(A("a1"), one(128), [[0, 8], [1, 16]], O.not_equal, 0.0, -15, 0)
+    iota(A("io0"), [[1, 256]], 0, 0)
+    iota(A("io1"), [[1, 256]], 1, 0)
+    tt(A("tmpb"), A("idb"), A("shu"), O.subtract)
+    tt(A("tmpb"), A("tmpb"), A("cor"), O.subtract)
+    ts(A("mid"), A("idb"), -1.0, O.mult)
+    fill(A("em"), 0.0)
+    for r in range(16):
+        act(A("em", 128 * r + r, 128 * r + 128, 16), A("blk", 0, 128, 16), F.Copy)
+    act(A("ep"), A("em"), F.Identity, scale=col(2))
+
+    def round_constants(t):
+        start = STEP * (t + 1)
+        m0 = start // 16
+        ml = m0 - 1
+        sel(A("ns%d" % t), A("tmpb"), [[1, 128]], O.not_equal, 0.0, -ml, 0)
+        sel(A("ni%d" % t), A("mid"), [[1, 128]], O.not_equal, 0.0, -ml, 0)
+        rr = "rr%d" % t
+        iota(A(rr, 0, ml), [[1, ml]], 128, 0)
+        iota(A(rr, m0, 128), [[1, 128 - m0]], m0, 0)
+        iota(A(rr, ml, m0), [[0, 1]], 126, 0)
+        ts(col(11), A("pcol"), float(m0), O.is_lt, 128.0, O.mult)
+        tt(col(12), col(11), A("pcol"), O.add)
+        ts(A("t1%d" % t), A(rr), col(12), O.is_ge)
+        sel(A("t2%d" % t), one(128), [[200, 128]], O.is_equal, 0.0, -127 - 200 * ml, 1)
+        sel(A("r0%d" % t), A("negb"), [[0, 256]], O.is_equal, 0.0, -m0, 1)
+        fill(A("lb%d" % t), 0.0)
+        sel(A("cw%d" % t), one(8), [[0, 8]], O.not_equal, -128.0, -ml, 1)
+        cp(A("lb%d" % t, 15, 1024, 144), A("cw%d" % t))
+
+    round_constants(0)
+    ts(A("sel15"), A("blk"), col(1), O.mult)
+    iota(A("iow"), [[16, 16]], 0, 0)
+    ts(A("iow"), A("iow"), col(0), O.add)
+    ts(A("iow1"), A("iow"), 1.0, O.add)
+    cp(A("id16"), A("idb"))
+
+    fill(A("tab", 2048, TW), 128.0 - K)
+    fill(A("cab", 2048, TW), 0.0)
+    for c in range(4):
+        s = 512 * c
+        ts(A("big", s, s + 512), A("detb", s, s + 512), 255, O.bitwise_and)
+        ts(A("df", s, s + 512), A("big", s, s + 512), 128.0, O.subtract)
+        act(A("cab", s, s + 512), A("df", s, s + 512), F.Abs)
+    for c in range(4):
+        s = 512 * c
+        mm(P(4 + c, 0, 512), A("blk"), A("cab", s, s + 512))
+        act(P(4 + c, 0, 512), P(4 + c, 0, 512), F.Sign, bias=-0.5)
+    act(A("cab", 2048, 2064), A("cab", 0, 16), F.Copy)
+    for c in range(4):
+        ts(A("tab", 512 * c, 512 * c + 512), A("detb", 512 * c, 512 * c + 512), float(K), O.subtract)
+
+    def rest_constants():
+        sel(A("rexp"), one(2048), [[-1, 128], [0, 16]], O.is_equal, 0.0, 0, 1)
+        ts(A("blk592"), A("blk", 0, 128, 16), 592.0, O.mult)
+        ts(A("w12", 0, 8), A("blk", 0, 128, 16), col(5), O.mult)
+        ts(A("w12", 8, 16), A("blk", 0, 128, 16), col(6), O.mult)
+        sel(A("kscan"), one(256), [[0, 16], [1, 16]], O.not_equal, -4.0e6, 0, 0)
+        sel(A("shd"), one(128), [[-1, 128]], O.is_equal, 0.0, 1, 1)
+        tt(A("gum"), A("idb"), A("shu"), O.subtract)
+        tt(A("gdm"), A("idb"), A("shd"), O.subtract)
+        sel(A("gum"), A("gum"), [[0, 8], [1, 16]], O.not_equal, 0.0, -15, 0)
+        sel(A("gdm"), A("gdm"), [[0, 8], [1, 16]], O.not_equal, 0.0, 0, 0)
+        cp(A("gu16"), A("gum"))
+        cp(A("gd16"), A("gdm"))
+        sel(A("rvkb"), one(512), [[-8, 4], [-1, 8], [0, 16]], O.is_equal, 0.0, 0, 1)
+        sel(A("trb"), A("blk"), [[-1, 128]], O.is_ge, 0.0, 0, 1)
+        ts(A("trb"), A("trb"), -1.0, O.mult)
+        iota(A("orow"), [[256, 5], [0, 16]], 0, 0)
+        sel(A("m80"), one(80), [[0, 5], [1, 16]], O.not_equal, 0.0, 0, 0)
+
+    def late_constants():
+        sel(A("bcb"), one(2048), [[-1, 16], [-16, 8], [0, 16]], O.is_equal, 0.0, 0, 1)
+        cp(A("bc"), A("bcb"))
+        iota(A("xio"), [[0, 16], [1, 16]], 0, 0)
+        ts(A("tm"), A("xio"), col(0), O.is_le, 0.5, O.mult)
+        for m in range(1, 8):
+            ts(A("mi", 128 * m, 128 * m + 128), A("idb"), 2.0 * m, O.mult)
+        iota(A("mc"), [[1, 8], [0, 16]], 0, 0)
+        ts(A("dumpc"), A("iow"), float(DUMP), O.add)
+        round_constants(1)
+        round_constants(2)
+
+    def whash(src):
+        for e in range(2):
+            for r in range(16):
+                mm(P(6, 16 * e, 16 * e + 16), A("e%d" % (e + 1), 128 * r, 128 * r + 128), A(src, r, 256, 16), r == 0, r == 15)
+        return None
+
+    def mix():
+        cp(A("ui"), P(6, 0, 32))
+        ts(A("ui2"), A("ui"), 4095, O.bitwise_and)
+        tt(A("pi"), A("ui2", 0, 16), A("ui2", 16, 32), O.mult)
+
+    def wsum(out, weights, src, c0, c1, start=True):
+        for r in range(16):
+            mm(out, A(weights, 128 * r, 128 * r + 128), A(src, c0 + r, c1, 16), start and r == 0, r == 15)
+
+    for t in range(RO):
+        start = STEP * (t + 1)
+        m0, off = start // 16, start % 16
+        last = t == RO - 1
+        for u in range(16):
+            mm(P(0, u, 128, 16), A("cab", off + u, off + u + 2033, 16), A("blk", 0, 128, 16))
+        mm(P(3, 0, 256), A("a1", 0, 128, 1, 0, 1), A("io1", 0, 256, 1, 0, 1), True, False)
+        ts(A("live"), P(0, 0, 128), 0.5, O.is_gt)
+        scan(A("w"), A("m128"), A("live"), O.mult, O.add)
+        mm(P(1, 0, 8), A("t1%d" % t), A("w", 15, 128, 16), True, False)
+        mm(P(1, 0, 8), A("t2%d" % t), A("w", 15 - off, 128, 16), False, True)
+        mm(P(2, 128, 136), A("ni%d" % t), A("w", 15, 128, 16))
+        mm(P(2, 0, 128), A("ns%d" % t), A("w"))
+        sel(A("wz"), A("w"), [[0, 8], [1, 16]], O.not_equal, 0.0, -15, 0)
+        act(A("cneg"), P(2, 128, 136), F.Copy)
+        lb = "lb%d" % t
+        for h in range(8):
+            ts(A("cmp", 256 * h, 256 * h + 256), A("io0"), P(1, h, h + 1), O.is_ge)
+            act(A(lb, 144 * h, 144 * h + 15), P(2, 16 * h, 16 * h + 15), F.Identity, bias=A("cneg", h, h + 1))
+            if h == 3:
+                mm(P(3, 0, 256), A("wz"), A("r0%d" % t), False, False)
+            mm(P(3, 0, 256), A(lb, 128 * h, 128 * h + 128), A("cmp", 256 * h, 256 * h + 256), False, h == 7)
+        if t == 0:
+            for c in range(4):
+                tt(A("tab", 512 * c, 512 * c + 512), A("tab", 512 * c, 512 * c + 512), P(4 + c, 0, 512), O.mult)
+        ts(A("val"), P(3, 0, 256), col(3), O.max, col(4), O.min)
+        mm(P(5, 0, 1), A("w"), A("ones", 0, 1))
+        act(A("totu"), P(5, 0, 1), F.Copy)
+        mm(P(5, 1, 2), A("sel15"), A("totu"))
+        ts(A("nx"), A("iow1"), P(5, 1, 2), O.subtract, 0.0, O.max)
+        ts(A("nt"), A("iow"), P(5, 1, 2), O.is_ge, float(DUMMY - start), O.mult)
+        if t == 0:
+            ts(A("e2"), A("em"), col(6), O.mult)
+        fill(A("sb%d" % t, 0, 1024), float(K + 128))
+        mm(P(4, 0, 16), A("id16"), A("nx"), True, False)
+        mm(P(4, 0, 16), A("id16"), A("nt"), False, False)
+        wsum(P(4, 0, 16), "ep", "val", 0, 256, False)
+        ts(A("pl"), P(4, 0, 16), float(16 * m0 + off), O.add)
+        if t == 0:
+            rest_constants()
+        cp(A("ti"), ind(A("tab"), A("pl")))
+        act(A("abc"), ind(A("cab"), A("pl")), F.Copy)
+        for h in range(2):
+            mm(P(7, 128 * h, 128 * h + 128), A("abc", 128 * h, 128 * h + 128), A("idb"))
+        ts(A("di"), A("ti"), 8, O.arith_shift_right, 4095, O.bitwise_and)
+        cp(A("du"), A("di"))
+        for a, b in ((0, 64), (64, 128), (128, 192), (192, 224)):
+            act(A("lg", 16 * a, 16 * b), ind(A("hamb"), A("du", a, b)), F.Copy)
+        cp(A("ct"), P(7, 0, 256))
+        ts(A("d16"), A("di"), 2048.0, O.subtract)
+        cp(A("lg", 3584, 4096), ind(A("hamb"), A("du", 224, 256)))
+        for h in range(2):
+            for e in range(2):
+                mm(P(4, 16 * e + 8 * h, 16 * e + 8 * h + 8), A("d16", 128 * h, 128 * h + 128), A("w12", 8 * e, 8 * e + 8))
+
+        def rep(b):
+            mm(P(b % 4, 0, 512), A("ct", 128 * (b // 4), 128 * (b // 4) + 128), A("rexp", 512 * (b % 4), 512 * (b % 4) + 512))
+
+        for b in range(4):
+            rep(b)
+        mm(P(7, 0, 256), A("gu16"), A("d16"))
+        mm(P(7, 256, 512), A("gd16"), A("d16"))
+        cp(A("ui"), P(4, 0, 32))
+        ts(A("ui2"), A("ui"), 4095, O.bitwise_and)
+        tt(A("pi"), A("ui2", 0, 16), A("ui2", 16, 32), O.mult)
+        ts(A("h16"), A("pi"), 1, O.arith_shift_right, 0x7FFFFFF0, O.bitwise_and)
+        ts(A("h16t"), A("h16"), float(16 * t), O.add)
+        for b in range(8):
+            s = 512 * b
+            tt(A("mn", s, s + 512), A("lg", s, s + 512), P(b % 4, 0, 512), O.min)
+            if b < 4:
+                rep(b + 4)
+            if b % 4 == 3:
+                h = b // 4
+                for k in range(16):
+                    mm(P(6, 128 * h + k, 128 * h + 128, 16), A("mn", 2048 * h + k, 2048 * h + 2048, 16), A("blk592"))
+        if t == 0:
+            ts(A("e1"), A("em"), col(5), O.mult)
+            cp(A("rvk"), A("rvkb"))
+            ts(A("rvk", 0, 256), A("rvk", 0, 256), -1.0, O.mult)
+        mm(P(5, 0, 256), A("id16"), A("d16"))
+        scan(A("km"), A("kscan"), P(6, 0, 256), O.add, O.max)
+        tt(A("si"), A("km", 15, 256, 16), A("h16t"), O.add)
+        ts(A("vk", 0, 16), A("si"), 4, O.arith_shift_right, 4095, O.bitwise_and)
+        ts(A("vk", 16, 32), A("si"), 15, O.bitwise_and)
+        ts(A("vk16"), A("vk"), 2048.0, O.subtract)
+        mm(P(4, 0, 128, 1, 0, 32), A("vk16"), A("id16"))
+        cp(A("t32", 0, 128, 1, 0, 32), P(4, 0, 128, 1, 0, 32))
+        ts(P(7, 0, 256), P(7, 0, 256), col(9), O.add)
+        ts(P(7, 256, 512), P(7, 256, 512), col(10), O.add)
+        for h in range(2):
+            s = 128 * h
+            mm(P(1, s, s + 128), A("rvk", 256 + s, 256 + s + 128, 1, 0, 32), A("t32", 0, 128, 1, 0, 32))
+        for h in range(2):
+            s = 128 * h
+            mm(P(0, s, s + 128), A("id16"), A("d16", s, s + 128), True, False)
+            mm(P(0, s, s + 128), A("rvk", s, s + 128, 1, 0, 32), A("t32", 0, 128, 1, 0, 32), False, True)
+        ts(A("ma"), P(1, 0, 256), col(7), O.is_ge)
+        act(A("mb"), P(1, 0, 256), F.Relu, bias=col(8), scale=-8192.0)
+        act(A("sd"), P(0, 0, 256), F.Sign)
+        wsum(P(3, 0, 16), "em", "sd", 0, 256)
+        tt(P(2, 0, 256), P(7, 0, 256), A("ma"), O.mult)
+        tt(A("lo"), P(7, 256, 512), A("mb"), O.min)
+        tt(A("t1"), A("lo"), P(0, 0, 256), O.min)
+        tt(A("tt"), A("t1"), P(2, 0, 256), O.max)
+        tt(A("ch16"), P(5, 0, 256), A("tt"), O.subtract)
+        act(A("st_"), A("tt"), F.Sign)
+        mm(P(5, 256, 512), A("blk"), A("st_"))
+        whash("ch16")
+        ts(A("fi"), A("ti"), 255, O.bitwise_and, 2, O.arith_shift_right)
+        ts(A("ff"), A("fi"), 32.0, O.subtract)
+        cp(A("vo"), P(3, 0, 16))
+        ts(A("vo2"), A("vo"), 1, O.bitwise_and)
+        tt(A("bad4"), A("vo2"), A("nt"), O.max)
+        ts(A("bad4"), A("bad4"), 0.0, O.is_gt, 4.0, O.mult)
+        ts(A("chp"), A("ch16"), 256.0, O.mult, 2048.0 * 256 + 128, O.add)
+        cp(A("npi"), P(5, 256, 512))
+        ts(A("npa"), A("npi"), 1, O.bitwise_and)
+        ts(A("q2"), A("npa"), 2.0, O.mult, -1.0, O.add)
+        tt(A("cq"), A("q2"), A("ff"), O.mult)
+        tt(A("pk"), A("chp"), A("cq"), O.add)
+        mix()
+        ts(A("own"), A("pi"), 5, O.arith_shift_right, 3, O.bitwise_and)
+        tt(A("own2"), A("own"), A("bad4"), O.max)
+        for o in range(5):
+            ts(A("oh", 16 * o, 16 * o + 16), A("own2"), float(o), O.is_equal)
+        mm(P(7, 80, 160), A("blk"), A("oh"))
+        mm(P(4, 0, 80), A("ones", 0, 128, 1, 0, 1), A("orow", 0, 80, 1, 0, 1), True, False)
+        mm(P(4, 0, 80), A("trb"), A("oh"), False, True)
+        scan(A("inc"), A("m80"), P(7, 80, 160), O.mult, O.add)
+        tt(A("rk"), A("inc"), P(4, 0, 80), O.add)
+        tt(A("mk"), A("rk"), A("oh"), O.mult)
+        for o in range(5):
+            mm(P(3, 0, 16), A("id16"), A("mk", 16 * o, 16 * o + 16), o == 0, o == 4)
+        cp(A("sl"), P(3, 0, 16))
+        sb, ar, arr = "sb%d" % t, "ar%d" % t, "arr%d" % t
+        cp(ind(A(sb), A("sl")), A("pk"))
+        trs = []
+        for o, es in plan(topo, T.cores, rank):
+            rid, pid = topo.addr(T.cores[o])[:2]
+            trs.append(RemoteDMATransfer(dst_ids=[DstId(rid=rid, pnc=pid)], dma_engine_mask=sum(1 << e for e in es), remote_sem=T.sem[arr],
+                                         src=A(sb, 256 * o, 256 * o + 64)[0], dst=A(ar, 64 * rank, 64 * rank + 64)[0]))
+        need("g", [], [A(sb)])
+        g.remote_dma_fused(trs, local_sem=T.sem.sent)
+        got = sum(len(es) for q in range(N) if q != rank for o, es in plan(topo, T.cores, q) if o == rank)
+        cp(A(ar, 64 * rank, 64 * rank + 64), A(sb, 256 * rank, 256 * rank + 64))
+        if t == 0:
+            late_constants()
+        ts(A("ci"), A("ti"), 255, O.bitwise_and)
+        ts(A("cc"), A("ci"), 128.0, O.subtract)
+        act(A("sgc"), A("cc"), F.Sign)
+        act(A("fa"), A("abc"), F.Relu, bias=-1.0)
+        mm(P(5, 0, 256), A("blk"), A("fa"))
+        act(A("fs"), P(5, 0, 256), F.Sign, bias=-0.5)
+        tt(A("fg"), A("ti"), A("sgc"), O.subtract)
+        tt(A("ft"), A("fg"), A("fs"), O.mult)
+        cp(ind(A("tab"), A("pl")), A("ft"))
+        if not last:
+            cp(ind(A("cab"), A("pl")), A("fa"))
+        ts(A("ai"), A(ar), 8, O.arith_shift_right, extra=[(arr, got)])
+        ts(A("a16"), A("ai"), 2048.0, O.subtract)
+        whash("a16")
+        ts(A("aa"), A("ai"), 256.0, O.mult, 128.0 - K, O.add)
+        ts(A("aam"), A("aa"), 256.0, O.subtract)
+        ts(A("ac"), A(ar), 255, O.bitwise_and)
+        mix()
+        ts(A("hu", 16, 32), A("ui2", 0, 16), 2048.0, O.subtract)
+        ts(A("hi_"), A("pi"), 7, O.arith_shift_right, 2047, O.bitwise_and)
+        cp(A("hu", 0, 16), A("hi_"))
+        for m in range(8):
+            if m:
+                mm(P(7, 16 * m, 16 * m + 16), A("mi", 128 * m, 128 * m + 128), A("hu", 16, 32), True, False)
+            mm(P(7, 16 * m, 16 * m + 16), A("id16"), A("hu", 0, 16), m == 0, True)
+        ts(A("sti"), A("ui2", 0, 16), 2.0, O.mult, 1.0, O.add)
+        tt(A("zi"), A("mc"), P(7, 0, 128), O.add)
+        ts(A("zi2"), A("zi"), 2047, O.bitwise_and)
+        cp(A("zu"), A("zi2"))
+        late = []
+        for m in range(8):
+            s = 256 * m
+            tt(A("df", s, s + 256), ind(A("tab"), A("zu", 16 * m, 16 * m + 16)), A("aa"), O.subtract)
+            act(A("ab", s, s + 256), A("df", s, s + 256), F.Abs)
+            while late:
+                z = late.pop()
+                ts(A("rl", z, z + 256), A("ab", z, z + 256), 127.0, O.subtract, 0.0, O.max)
+            if m in (1, 4, 6):
+                late.append(s)
+            else:
+                act(A("rl", s, s + 256), A("ab", s, s + 256), F.Relu, bias=-127.0)
+            if m % 4 == 3:
+                wsum(P(m // 4, 0, 64), "em", "rl", 256 * m - 768, 256 * m + 256)
+        for h in range(2):
+            a, b = 64 * h, 64 * h + 64
+            ts(A("k1", a, b), P(h, 0, 64), 0.5, O.is_gt, 16.0, O.mult)
+            ts(A("k2", a, b), P(h, 0, 64), 8.4e7, O.is_gt, -8.0, O.mult)
+            tt(A("k1", a, b), A("k1", a, b), A("mc", a, b), O.add)
+            tt(A("k3", a, b), A("k1", a, b), A("k2", a, b), O.add)
+        tt(A("k4"), A("k3", 0, 64), A("k3", 64, 128), O.min)
+        tt(A("k5"), A("k4", 0, 32), A("k4", 32, 64), O.min)
+        tt(A("kmi"), A("k5", 0, 16), A("k5", 16, 32), O.min)
+        ts(A("m7"), A("kmi"), 7, O.bitwise_and)
+        ts(A("inv"), A("kmi"), 16.0, O.is_ge, -4096.0, O.mult)
+        tt(A("ms"), A("m7"), A("sti"), O.mult)
+        tt(A("msz"), A("ms"), A("hi_"), O.add)
+        ts(A("plc"), A("msz"), 2047, O.bitwise_and)
+        tt(A("key16"), A("plc"), A("inv"), O.add)
+        tt(A("keyw"), A("plc"), A("inv"), O.add)
+        cp(A("plu"), A("plc"))
+        mm(P(3, 0, 256), A("blk"), A("zb"), True, False)
+        for r in range(16):
+            mm(P(2, r, 256, 16), A("bc", 128 * r, 128 * r + 128), A("key16"))
+        cp(A("oi"), ind(A("tab"), A("plu")))
+        ts(A("oc"), A("oi"), 255, O.bitwise_and)
+        mm(P(6, 0, 256), A("id16"), A("tm"), True, False)
+        for x in range(16):
+            mm(P(6, x, 256, 16), A("id16"), A("key16"), False, x == 15)
+        cp(A("kb16"), P(2, 0, 256))
+        for c in range(15):
+            e = A("eq", 256 * c + 16 * c + 16, 256 * c + 256)
+            ts(e, A("kb16", 16 * c + 16, 256), A("keyw", c, c + 1), O.is_equal)
+            mm(P(3, 16 * c + 16, 256), A("blk"), e, False, False)
+            if c == 9:
+                tt(A("dm"), P(6, 0, 256), A("kb16"), O.is_equal)
+        mm(P(3, 0, 256), A("blk"), A("dm"), False, True)
+        tt(A("cs"), A("oc"), A("ac"), O.add)
+        act(A("lsb"), P(3, 0, 256), F.Copy)
+        ts(A("cn"), A("cs"), 129.0, O.max, 383.0, O.min)
+        act(A("ent"), A("cn"), F.Abs, bias=-256.0)
+        mm(P(5, 0, 256), A("blk"), A("ent"))
+        wsum(P(4, 0, 16), "em", "lsb", 0, 256)
+        tt(A("tg"), A("aam"), A("cn"), O.add)
+        act(A("es"), P(5, 0, 256), F.Sign, bias=-0.5)
+        tt(A("tn"), A("tg"), A("es"), O.mult)
+        tt(A("ls"), A("inv"), P(4, 0, 16), O.subtract)
+        ts(A("ls2"), A("ls"), -0.5, O.is_lt)
+        tt(A("ls"), A("ls2"), A("dumpc"), O.mult)
+        tt(A("fo"), A("ls"), A("plc"), O.max)
+        cp(A("fou"), A("fo"))
+        if not last:
+            cp(ind(A("cab"), A("fou")), A("ent"))
+            cp(A("cab", 2048, 2064), A("cab", 0, 16))
+        cp(ind(A("tab"), A("fou")), A("tn"))
+
+    for c in range(4):
+        s = 512 * c
+        act(A("ab", s, s + 512), A("tab", s, s + 512), F.Abs)
+        ts(A("df", s, s + 512), A("ab", s, s + 512), -1.0, O.mult, float(K), O.add)
+        store("y", "out%d" % c, T.y[:, s:s + 512], A("df", s, s + 512))
+    for c in range(4):
+        g.wait_ge(T.sem["out%d" % c], 16)
+    g.wait_ge(T.sem.ldh, 16)
+    g.wait_ge(T.sem.sent, 8 * RO)
+    for q in ("v", "s", "t", "g"):
+        g.wait_ge(T.sem[SEMOF[q]], count[q])

@@ -2,6 +2,7 @@ from concourse.bass import DstId, RemoteDMATransfer
 from concourse.mybir import AluOpType as O, ActivationFunctionType as F
 
 RO, STEP, N, CAP = 3, 650, 4, 64
+CH = ((0, 64), (64, 128), (128, 192), (192, 224), (224, 256))
 TW = 2576
 DUMMY, DUMP = 2064, 2320
 K = 1 << 22
@@ -11,22 +12,22 @@ WIDE = {
     "detb": (2048, I32), "big": (2048, I32), "tab": (TW, F32), "cab": (TW, B16), "hamb": (4096, B16), "ones": (2048, B16),
     "em": (2048, B16), "ep": (2048, B16), "e1": (2048, H16), "e2": (2048, H16), "bcb": (2048, B16), "bc": (2048, H16),
     "rexp": (2048, B16), "lb0": (1024, B16), "lb1": (1024, B16), "lb2": (1024, B16), "rvkb": (512, B16), "rvk": (512, H16),
-    "mi": (1024, H16), "cmp": (2048, B16), "lg": (4096, B16), "mn": (4096, B16), "sb0": (1280, I32), "sb1": (1280, I32),
-    "sb2": (1280, I32), "ar0": (256, I32), "ar1": (256, I32), "ar2": (256, I32), "df": (2048, F32), "ab": (2048, F32),
-    "rl": (2048, B16), "eq": (4096, B16),
+    "cmp": (2048, B16), "lg": (4096, B16), "mn": (4096, B16), "sb0": (1280, I32), "sb1": (1280, I32), "sb2": (1280, I32),
+    "ar0": (256, I32), "ar1": (256, I32), "ar2": (256, I32), "df": (2048, F32), "ab": (2048, F32), "rl": (2048, B16),
+    "eq": (4096, B16),
 }
 SMALL = {
-    F32: "pcol 1 cols 16 rr0 128 rr1 128 rr2 128 cw0 8 cw1 8 cw2 8 kscan 256 m80 80 sel15 128 iow 16 iow1 16 xio 256 mc 128 "
-         "dumpc 16 cneg 8 totu 1 bad4 16 cc 256 sgc 256 ff 256 km 256 ma 256 mb 256 lo 256 t1 256 tt 256 own2 16 inc 80 rk 80 "
-         "q2 256 cq 256 chp 256 pk 256 fs 256 fg 256 ft 256 aa 256 aam 256 k1 128 k2 128 k3 128 k4 64 k5 32 inv 16 keyw 16 "
-         "cs 256 cn 256 tg 256 tn 256 es 256 ls 16 ls2 16 fo 16",
+    F32: "pcol 1 cols 16 rr0 128 rr1 128 rr2 128 cw0 8 cw1 8 cw2 8 kscan 256 m80 80 sel15 128 iow 16 iow1 16 xio 16 tm 16 kr 256 "
+         "mc 128 dumpc 16 cneg 8 totu 1 bad4 16 cc 256 sgc 256 ff 256 km 256 ma 256 mb 256 lo 256 t1 256 tt 256 own2 16 inc 80 "
+         "rk 80 q2 256 cq 256 chp 256 pk 256 fs 256 fg 256 ft 256 aa 256 aam 256 st1 16 st2 32 st4 64 mz 128 k1 128 k2 128 "
+         "k3 128 k4 64 k5 32 inv 16 keyw 16 cs 256 cn 256 tg 256 tn 256 es 256 ls 16 ls2 16 fo 16",
     B16: "blk 128 blk592 8 idb 128 shu 128 shd 128 cor 128 tmpb 128 mid 128 gum 128 gdm 128 ns0 128 ns1 128 ns2 128 ni0 128 "
          "ni1 128 ni2 128 t10 128 t11 128 t12 128 t20 128 t21 128 t22 128 r00 256 r01 256 r02 256 negb 256 io0 256 io1 256 "
          "a1 128 m128 128 trb 128 orow 80 zb 256 live 128 w 128 wz 128 val 256 abc 256 ct 256 sd 256 st_ 256 oh 80 fa 256 "
          "ent 256 dm 256 lsb 256",
-    H16: "id16 128 gu16 128 gd16 128 w12 16 tm 256 nx 16 nt 16 d16 256 vk16 32 t32 128 ch16 256 mk 80 a16 256 hu 32 key16 16 kb16 256",
-    I32: "icol 1 icol2 1 ti 256 di 256 ci 256 fi 256 ui 32 ui2 32 pi 16 h16 16 h16t 16 si 16 vk 32 vo 16 vo2 16 own 16 npi 256 "
-         "npa 256 ai 256 ac 256 hi_ 16 sti 16 zi 128 zi2 128 kmi 16 m7 16 ms 16 msz 16 plc 16 oi 256 oc 256",
+    H16: "id16 128 gu16 128 gd16 128 w12 16 nx 16 nt 16 d16 256 vk16 32 t32 128 ch16 256 mk 80 a16 256 key16 16 kb16 256",
+    I32: "icol 1 icol2 1 ti 256 ci 256 fi 256 ui 32 ui2 32 pi 16 h16 16 h16t 16 si 16 vk 32 vo 16 vo2 16 own 16 npi 256 "
+         "npa 256 ai 256 ac 256 z 128 zi2 128 kmi 16 plc 16 oi 256 oc 256",
     U16: "pl 16 du 256 sl 16 zu 128 plu 16 fou 16",
 }
 
@@ -191,7 +192,8 @@ def rank_program(g, core, T, topo):
         load("y", "ld%d" % c, A("detb", 512 * c, 512 * c + 512), T.det[:, 512 * c:512 * c + 512])
     load("s", "ldh", A("hamb"), T.ham[:, :])
 
-    fill(A("ones"), 1.0)
+    fill(A("ones", 0, 256), 1.0)
+    fill(A("em"), 0.0)
     iota(A("icol"), [[0, 1]], 0, 1)
     sel(A("tmpb"), one(128), [[-16, 8], [0, 16]], O.is_ge, 0.0, 0, 1)
     sel(A("blk"), A("tmpb"), [[16, 8], [0, 16]], O.is_ge, 0.0, 15, -1)
@@ -202,13 +204,10 @@ def rank_program(g, core, T, topo):
     ts(col(2), col(1), 15.0, O.mult, 1.0, O.add)
     ts(col(3), col(1), -1000.0, O.mult)
     ts(col(4), col(1), 999.0, O.mult, 1.0, O.add)
-    ts(col(5), col(0), 13.0, O.mult, 5.0, O.add)
-    ts(col(6), col(0), -14.0, O.mult, 255.0, O.add)
-    ts(col(7), col(0), -1.0, O.mult, -2033.0, O.add)
-    ts(col(8), col(7), 8192.0, O.mult, 8192.0, O.add)
-    ts(col(9), col(1), -8192.0, O.mult)
-    ts(col(10), col(0), 0.0, O.is_equal, 8192.0, O.mult)
-    fill(A("zb"), 0.0)
+    fill(A("ones", 256, 2048), 1.0)
+    for r in range(16):
+        act(A("em", 128 * r + r, 128 * r + 128, 16), A("blk", 0, 128, 16), F.Copy)
+    act(A("ep"), A("em"), F.Identity, scale=col(2))
     fill(A("negb"), -1.0)
     sel(A("idb"), one(128), [[-1, 128]], O.is_equal, 0.0, 0, 1)
     sel(A("shu"), one(128), [[-1, 128]], O.is_equal, 0.0, -1, 1)
@@ -217,13 +216,16 @@ def rank_program(g, core, T, topo):
     sel(A("a1"), one(128), [[0, 8], [1, 16]], O.not_equal, 0.0, -15, 0)
     iota(A("io0"), [[1, 256]], 0, 0)
     iota(A("io1"), [[1, 256]], 1, 0)
-    tt(A("tmpb"), A("idb"), A("shu"), O.subtract)
-    tt(A("tmpb"), A("tmpb"), A("cor"), O.subtract)
-    ts(A("mid"), A("idb"), -1.0, O.mult)
-    fill(A("em"), 0.0)
-    for r in range(16):
-        act(A("em", 128 * r + r, 128 * r + 128, 16), A("blk", 0, 128, 16), F.Copy)
-    act(A("ep"), A("em"), F.Identity, scale=col(2))
+    for c in range(4):
+        s = 512 * c
+        ts(A("big", s, s + 512), A("detb", s, s + 512), 255, O.bitwise_and)
+        ts(A("df", s, s + 512), A("big", s, s + 512), 128.0, O.subtract)
+        act(A("cab", s, s + 512), A("df", s, s + 512), F.Abs)
+        if c == 0:
+            tt(A("tmpb"), A("idb"), A("shu"), O.subtract)
+            tt(A("tmpb"), A("tmpb"), A("cor"), O.subtract)
+            ts(A("mid"), A("idb"), -1.0, O.mult)
+    act(A("cab", 2048, 2064), A("cab", 0, 16), F.Copy)
 
     def round_constants(t):
         start = STEP * (t + 1)
@@ -251,61 +253,54 @@ def rank_program(g, core, T, topo):
     ts(A("iow1"), A("iow"), 1.0, O.add)
     cp(A("id16"), A("idb"))
 
-    fill(A("tab", 2048, TW), 128.0 - K)
-    fill(A("cab", 2048, TW), 0.0)
-    for c in range(4):
-        s = 512 * c
-        ts(A("big", s, s + 512), A("detb", s, s + 512), 255, O.bitwise_and)
-        ts(A("df", s, s + 512), A("big", s, s + 512), 128.0, O.subtract)
-        act(A("cab", s, s + 512), A("df", s, s + 512), F.Abs)
-    for c in range(4):
-        s = 512 * c
-        mm(P(4 + c, 0, 512), A("blk"), A("cab", s, s + 512))
-        act(P(4 + c, 0, 512), P(4 + c, 0, 512), F.Sign, bias=-0.5)
-    act(A("cab", 2048, 2064), A("cab", 0, 16), F.Copy)
-    for c in range(4):
-        ts(A("tab", 512 * c, 512 * c + 512), A("detb", 512 * c, 512 * c + 512), float(K), O.subtract)
-
-    def rest_constants():
+    def rest_g():
+        sel(A("kscan"), one(256), [[0, 16], [1, 16]], O.not_equal, -4.0e6, 0, 0)
+        sel(A("shd"), one(128), [[-1, 128]], O.is_equal, 0.0, 1, 1)
+        sel(A("rvkb"), one(512), [[-8, 4], [-1, 8], [0, 16]], O.is_equal, 0.0, 0, 1)
+        sel(A("trb"), A("blk"), [[-1, 128]], O.is_ge, 0.0, 0, 1)
+        iota(A("mc"), [[2048, 8], [0, 16]], 0, 0)
+        iota(A("orow"), [[256, 5], [0, 16]], 0, 0)
+        sel(A("m80"), one(80), [[0, 5], [1, 16]], O.not_equal, 0.0, 0, 0)
         sel(A("rexp"), one(2048), [[-1, 128], [0, 16]], O.is_equal, 0.0, 0, 1)
+        sel(A("bcb"), one(2048), [[-1, 16], [-16, 8], [0, 16]], O.is_equal, 0.0, 0, 1)
+
+    def rest_v():
+        ts(col(5), col(0), 13.0, O.mult, 5.0, O.add)
+        ts(col(6), col(0), -14.0, O.mult, 255.0, O.add)
+        ts(col(7), col(0), -1.0, O.mult, -2033.0, O.add)
+        ts(col(8), col(7), 8192.0, O.mult, 8192.0, O.add)
+        ts(col(9), col(1), -8192.0, O.mult)
+        ts(col(10), col(0), 0.0, O.is_equal, 8192.0, O.mult)
+        fill(A("zb"), 0.0)
         ts(A("blk592"), A("blk", 0, 128, 16), 592.0, O.mult)
         ts(A("w12", 0, 8), A("blk", 0, 128, 16), col(5), O.mult)
         ts(A("w12", 8, 16), A("blk", 0, 128, 16), col(6), O.mult)
-        sel(A("kscan"), one(256), [[0, 16], [1, 16]], O.not_equal, -4.0e6, 0, 0)
-        sel(A("shd"), one(128), [[-1, 128]], O.is_equal, 0.0, 1, 1)
         tt(A("gum"), A("idb"), A("shu"), O.subtract)
         tt(A("gdm"), A("idb"), A("shd"), O.subtract)
-        sel(A("gum"), A("gum"), [[0, 8], [1, 16]], O.not_equal, 0.0, -15, 0)
-        sel(A("gdm"), A("gdm"), [[0, 8], [1, 16]], O.not_equal, 0.0, 0, 0)
-        cp(A("gu16"), A("gum"))
-        cp(A("gd16"), A("gdm"))
-        sel(A("rvkb"), one(512), [[-8, 4], [-1, 8], [0, 16]], O.is_equal, 0.0, 0, 1)
-        sel(A("trb"), A("blk"), [[-1, 128]], O.is_ge, 0.0, 0, 1)
+        tt(A("gu16"), A("gum"), A("a1"), O.mult)
+        tt(A("gd16"), A("gdm"), A("m128"), O.mult)
         ts(A("trb"), A("trb"), -1.0, O.mult)
-        iota(A("orow"), [[256, 5], [0, 16]], 0, 0)
-        sel(A("m80"), one(80), [[0, 5], [1, 16]], O.not_equal, 0.0, 0, 0)
 
     def late_constants():
-        sel(A("bcb"), one(2048), [[-1, 16], [-16, 8], [0, 16]], O.is_equal, 0.0, 0, 1)
         cp(A("bc"), A("bcb"))
-        iota(A("xio"), [[0, 16], [1, 16]], 0, 0)
+        iota(A("xio"), [[1, 16]], 0, 0)
         ts(A("tm"), A("xio"), col(0), O.is_le, 0.5, O.mult)
-        for m in range(1, 8):
-            ts(A("mi", 128 * m, 128 * m + 128), A("idb"), 2.0 * m, O.mult)
-        iota(A("mc"), [[1, 8], [0, 16]], 0, 0)
         ts(A("dumpc"), A("iow"), float(DUMP), O.add)
-        round_constants(1)
-        round_constants(2)
 
     def whash(src):
         for e in range(2):
             for r in range(16):
                 mm(P(6, 16 * e, 16 * e + 16), A("e%d" % (e + 1), 128 * r, 128 * r + 128), A(src, r, 256, 16), r == 0, r == 15)
-        return None
 
-    def mix():
+    def mix(steps=False):
         cp(A("ui"), P(6, 0, 32))
         ts(A("ui2"), A("ui"), 4095, O.bitwise_and)
+        if steps:
+            ts(A("st1"), A("ui2", 0, 16), 2.0, O.mult, 1.0, O.add)
+            for j in range(2):
+                act(A("st2", 16 * j, 16 * j + 16), A("st1"), F.Identity, scale=2.0)
+            for j in range(2):
+                act(A("st4", 32 * j, 32 * j + 32), A("st2"), F.Identity, scale=2.0)
         tt(A("pi"), A("ui2", 0, 16), A("ui2", 16, 32), O.mult)
 
     def wsum(out, weights, src, c0, c1, start=True):
@@ -319,13 +314,20 @@ def rank_program(g, core, T, topo):
         for u in range(16):
             mm(P(0, u, 128, 16), A("cab", off + u, off + u + 2033, 16), A("blk", 0, 128, 16))
         mm(P(3, 0, 256), A("a1", 0, 128, 1, 0, 1), A("io1", 0, 256, 1, 0, 1), True, False)
+        if t == 0:
+            ts(A("tab", 0, 512), A("detb", 0, 512), float(K), O.subtract)
         ts(A("live"), P(0, 0, 128), 0.5, O.is_gt)
         scan(A("w"), A("m128"), A("live"), O.mult, O.add)
+        if t == 0:
+            for c in range(1, 4):
+                ts(A("tab", 512 * c, 512 * c + 512), A("detb", 512 * c, 512 * c + 512), float(K), O.subtract)
         mm(P(1, 0, 8), A("t1%d" % t), A("w", 15, 128, 16), True, False)
         mm(P(1, 0, 8), A("t2%d" % t), A("w", 15 - off, 128, 16), False, True)
         mm(P(2, 128, 136), A("ni%d" % t), A("w", 15, 128, 16))
         mm(P(2, 0, 128), A("ns%d" % t), A("w"))
         sel(A("wz"), A("w"), [[0, 8], [1, 16]], O.not_equal, 0.0, -15, 0)
+        if t == 0:
+            rest_g()
         act(A("cneg"), P(2, 128, 136), F.Copy)
         lb = "lb%d" % t
         for h in range(8):
@@ -335,34 +337,34 @@ def rank_program(g, core, T, topo):
                 mm(P(3, 0, 256), A("wz"), A("r0%d" % t), False, False)
             mm(P(3, 0, 256), A(lb, 128 * h, 128 * h + 128), A("cmp", 256 * h, 256 * h + 256), False, h == 7)
         if t == 0:
+            rest_v()
+            fill(A("tab", 2048, TW), 128.0 - K)
+            fill(A("cab", 2064, TW), 0.0)
             for c in range(4):
-                tt(A("tab", 512 * c, 512 * c + 512), A("tab", 512 * c, 512 * c + 512), P(4 + c, 0, 512), O.mult)
+                s = 512 * c
+                mm(P(4 + c, 0, 512), A("blk"), A("cab", s, s + 512))
+                act(P(4 + c, 0, 512), P(4 + c, 0, 512), F.Sign, bias=-0.5)
+                tt(A("tab", s, s + 512), A("tab", s, s + 512), P(4 + c, 0, 512), O.mult)
         ts(A("val"), P(3, 0, 256), col(3), O.max, col(4), O.min)
         mm(P(5, 0, 1), A("w"), A("ones", 0, 1))
         act(A("totu"), P(5, 0, 1), F.Copy)
         mm(P(5, 1, 2), A("sel15"), A("totu"))
         ts(A("nx"), A("iow1"), P(5, 1, 2), O.subtract, 0.0, O.max)
         ts(A("nt"), A("iow"), P(5, 1, 2), O.is_ge, float(DUMMY - start), O.mult)
-        if t == 0:
-            ts(A("e2"), A("em"), col(6), O.mult)
         fill(A("sb%d" % t, 0, 1024), float(K + 128))
         mm(P(4, 0, 16), A("id16"), A("nx"), True, False)
         mm(P(4, 0, 16), A("id16"), A("nt"), False, False)
         wsum(P(4, 0, 16), "ep", "val", 0, 256, False)
         ts(A("pl"), P(4, 0, 16), float(16 * m0 + off), O.add)
-        if t == 0:
-            rest_constants()
-        cp(A("ti"), ind(A("tab"), A("pl")))
+        ts(A("du"), ind(A("tab"), A("pl")), 1.0 / 256, O.mult, K / 256 - 0.5, O.add)
         act(A("abc"), ind(A("cab"), A("pl")), F.Copy)
         for h in range(2):
             mm(P(7, 128 * h, 128 * h + 128), A("abc", 128 * h, 128 * h + 128), A("idb"))
-        ts(A("di"), A("ti"), 8, O.arith_shift_right, 4095, O.bitwise_and)
-        cp(A("du"), A("di"))
-        for a, b in ((0, 64), (64, 128), (128, 192), (192, 224)):
+        for a, b in CH:
             act(A("lg", 16 * a, 16 * b), ind(A("hamb"), A("du", a, b)), F.Copy)
+        ts(A("d16"), A("du"), 2048.0, O.subtract)
         cp(A("ct"), P(7, 0, 256))
-        ts(A("d16"), A("di"), 2048.0, O.subtract)
-        cp(A("lg", 3584, 4096), ind(A("hamb"), A("du", 224, 256)))
+        cp(A("ti"), ind(A("tab"), A("pl")))
         for h in range(2):
             for e in range(2):
                 mm(P(4, 16 * e + 8 * h, 16 * e + 8 * h + 8), A("d16", 128 * h, 128 * h + 128), A("w12", 8 * e, 8 * e + 8))
@@ -390,8 +392,17 @@ def rank_program(g, core, T, topo):
                     mm(P(6, 128 * h + k, 128 * h + 128, 16), A("mn", 2048 * h + k, 2048 * h + 2048, 16), A("blk592"))
         if t == 0:
             ts(A("e1"), A("em"), col(5), O.mult)
+            ts(A("e2"), A("em"), col(6), O.mult)
             cp(A("rvk"), A("rvkb"))
             ts(A("rvk", 0, 256), A("rvk", 0, 256), -1.0, O.mult)
+        ts(A("fi"), A("ti"), 255, O.bitwise_and, 2, O.arith_shift_right)
+        ts(A("ff"), A("fi"), 32.0, O.subtract)
+        ts(A("ci"), A("ti"), 255, O.bitwise_and)
+        ts(A("cc"), A("ci"), 128.0, O.subtract)
+        act(A("sgc"), A("cc"), F.Sign)
+        act(A("fa"), A("abc"), F.Relu, bias=-1.0)
+        mm(P(3, 0, 256), A("blk"), A("fa"))
+        act(A("fs"), P(3, 0, 256), F.Sign, bias=-0.5)
         mm(P(5, 0, 256), A("id16"), A("d16"))
         scan(A("km"), A("kscan"), P(6, 0, 256), O.add, O.max)
         tt(A("si"), A("km", 15, 256, 16), A("h16t"), O.add)
@@ -421,8 +432,6 @@ def rank_program(g, core, T, topo):
         act(A("st_"), A("tt"), F.Sign)
         mm(P(5, 256, 512), A("blk"), A("st_"))
         whash("ch16")
-        ts(A("fi"), A("ti"), 255, O.bitwise_and, 2, O.arith_shift_right)
-        ts(A("ff"), A("fi"), 32.0, O.subtract)
         cp(A("vo"), P(3, 0, 16))
         ts(A("vo2"), A("vo"), 1, O.bitwise_and)
         tt(A("bad4"), A("vo2"), A("nt"), O.max)
@@ -458,36 +467,24 @@ def rank_program(g, core, T, topo):
         g.remote_dma_fused(trs, local_sem=T.sem.sent)
         got = sum(len(es) for q in range(N) if q != rank for o, es in plan(topo, T.cores, q) if o == rank)
         cp(A(ar, 64 * rank, 64 * rank + 64), A(sb, 256 * rank, 256 * rank + 64))
-        if t == 0:
-            late_constants()
-        ts(A("ci"), A("ti"), 255, O.bitwise_and)
-        ts(A("cc"), A("ci"), 128.0, O.subtract)
-        act(A("sgc"), A("cc"), F.Sign)
-        act(A("fa"), A("abc"), F.Relu, bias=-1.0)
-        mm(P(5, 0, 256), A("blk"), A("fa"))
-        act(A("fs"), P(5, 0, 256), F.Sign, bias=-0.5)
         tt(A("fg"), A("ti"), A("sgc"), O.subtract)
         tt(A("ft"), A("fg"), A("fs"), O.mult)
         cp(ind(A("tab"), A("pl")), A("ft"))
         if not last:
             cp(ind(A("cab"), A("pl")), A("fa"))
+            fill(A("tab", 2048, DUMP), 128.0 - K)
         ts(A("ai"), A(ar), 8, O.arith_shift_right, extra=[(arr, got)])
         ts(A("a16"), A("ai"), 2048.0, O.subtract)
         whash("a16")
         ts(A("aa"), A("ai"), 256.0, O.mult, 128.0 - K, O.add)
         ts(A("aam"), A("aa"), 256.0, O.subtract)
         ts(A("ac"), A(ar), 255, O.bitwise_and)
-        mix()
-        ts(A("hu", 16, 32), A("ui2", 0, 16), 2048.0, O.subtract)
-        ts(A("hi_"), A("pi"), 7, O.arith_shift_right, 2047, O.bitwise_and)
-        cp(A("hu", 0, 16), A("hi_"))
-        for m in range(8):
-            if m:
-                mm(P(7, 16 * m, 16 * m + 16), A("mi", 128 * m, 128 * m + 128), A("hu", 16, 32), True, False)
-            mm(P(7, 16 * m, 16 * m + 16), A("id16"), A("hu", 0, 16), m == 0, True)
-        ts(A("sti"), A("ui2", 0, 16), 2.0, O.mult, 1.0, O.add)
-        tt(A("zi"), A("mc"), P(7, 0, 128), O.add)
-        ts(A("zi2"), A("zi"), 2047, O.bitwise_and)
+        mix(True)
+        ts(A("z", 0, 16), A("pi"), 7, O.arith_shift_right, 2047, O.bitwise_and)
+        tt(A("z", 16, 32), A("z", 0, 16), A("st1"), O.add)
+        tt(A("z", 32, 64), A("z", 0, 32), A("st2"), O.add)
+        tt(A("z", 64, 128), A("z", 0, 64), A("st4"), O.add)
+        ts(A("zi2"), A("z"), 2047, O.bitwise_and)
         cp(A("zu"), A("zi2"))
         late = []
         for m in range(8):
@@ -497,26 +494,26 @@ def rank_program(g, core, T, topo):
             while late:
                 z = late.pop()
                 ts(A("rl", z, z + 256), A("ab", z, z + 256), 127.0, O.subtract, 0.0, O.max)
-            if m in (1, 4, 6):
+            if m % 2 == 0:
                 late.append(s)
             else:
                 act(A("rl", s, s + 256), A("ab", s, s + 256), F.Relu, bias=-127.0)
             if m % 4 == 3:
                 wsum(P(m // 4, 0, 64), "em", "rl", 256 * m - 768, 256 * m + 256)
+        tt(A("mz"), A("mc"), A("zi2"), O.add)
+        if t == 0:
+            late_constants()
         for h in range(2):
             a, b = 64 * h, 64 * h + 64
-            ts(A("k1", a, b), P(h, 0, 64), 0.5, O.is_gt, 16.0, O.mult)
-            ts(A("k2", a, b), P(h, 0, 64), 8.4e7, O.is_gt, -8.0, O.mult)
-            tt(A("k1", a, b), A("k1", a, b), A("mc", a, b), O.add)
+            ts(A("k1", a, b), P(h, 0, 64), 0.5, O.is_gt, 32768.0, O.mult)
+            ts(A("k2", a, b), P(h, 0, 64), 8.4e7, O.is_gt, -16384.0, O.mult)
+            tt(A("k1", a, b), A("k1", a, b), A("mz", a, b), O.add)
             tt(A("k3", a, b), A("k1", a, b), A("k2", a, b), O.add)
         tt(A("k4"), A("k3", 0, 64), A("k3", 64, 128), O.min)
         tt(A("k5"), A("k4", 0, 32), A("k4", 32, 64), O.min)
         tt(A("kmi"), A("k5", 0, 16), A("k5", 16, 32), O.min)
-        ts(A("m7"), A("kmi"), 7, O.bitwise_and)
-        ts(A("inv"), A("kmi"), 16.0, O.is_ge, -4096.0, O.mult)
-        tt(A("ms"), A("m7"), A("sti"), O.mult)
-        tt(A("msz"), A("ms"), A("hi_"), O.add)
-        ts(A("plc"), A("msz"), 2047, O.bitwise_and)
+        ts(A("inv"), A("kmi"), 32768.0, O.is_ge, -4096.0, O.mult)
+        ts(A("plc"), A("kmi"), 2047, O.bitwise_and)
         tt(A("key16"), A("plc"), A("inv"), O.add)
         tt(A("keyw"), A("plc"), A("inv"), O.add)
         cp(A("plu"), A("plc"))
@@ -525,16 +522,15 @@ def rank_program(g, core, T, topo):
             mm(P(2, r, 256, 16), A("bc", 128 * r, 128 * r + 128), A("key16"))
         cp(A("oi"), ind(A("tab"), A("plu")))
         ts(A("oc"), A("oi"), 255, O.bitwise_and)
-        mm(P(6, 0, 256), A("id16"), A("tm"), True, False)
         for x in range(16):
-            mm(P(6, x, 256, 16), A("id16"), A("key16"), False, x == 15)
+            act(A("kr", x, 256, 16), A("keyw"), F.Identity, bias=A("tm", x, x + 1))
         cp(A("kb16"), P(2, 0, 256))
         for c in range(15):
             e = A("eq", 256 * c + 16 * c + 16, 256 * c + 256)
             ts(e, A("kb16", 16 * c + 16, 256), A("keyw", c, c + 1), O.is_equal)
             mm(P(3, 16 * c + 16, 256), A("blk"), e, False, False)
-            if c == 9:
-                tt(A("dm"), P(6, 0, 256), A("kb16"), O.is_equal)
+            if c == 13:
+                tt(A("dm"), A("kr"), A("kb16"), O.is_equal)
         mm(P(3, 0, 256), A("blk"), A("dm"), False, True)
         tt(A("cs"), A("oc"), A("ac"), O.add)
         act(A("lsb"), P(3, 0, 256), F.Copy)
@@ -545,6 +541,8 @@ def rank_program(g, core, T, topo):
         tt(A("tg"), A("aam"), A("cn"), O.add)
         act(A("es"), P(5, 0, 256), F.Sign, bias=-0.5)
         tt(A("tn"), A("tg"), A("es"), O.mult)
+        if not last:
+            round_constants(t + 1)
         tt(A("ls"), A("inv"), P(4, 0, 16), O.subtract)
         ts(A("ls2"), A("ls"), -0.5, O.is_lt)
         tt(A("ls"), A("ls2"), A("dumpc"), O.mult)

@@ -2,7 +2,7 @@ from concourse.bass import DstId, RemoteDMATransfer
 from concourse.mybir import AluOpType as O, ActivationFunctionType as F
 
 RO, STEP, N, CAP = 3, 650, 4, 64
-CH = ((0, 64), (64, 128), (128, 192), (192, 224), (224, 256))
+CH = ((0, 64), (64, 128), (128, 192), (192, 224))
 TW = 2576
 DUMMY, DUMP = 2064, 2320
 K = 1 << 22
@@ -10,22 +10,21 @@ F32, B16, H16, I32, U16 = "float32", "bfloat16", "float16", "int32", "uint16"
 
 WIDE = {
     "detb": (2048, I32), "big": (2048, I32), "tab": (TW, F32), "cab": (TW, B16), "hamb": (4096, B16), "ones": (2048, B16),
-    "em": (2048, B16), "ep": (2048, B16), "e1": (2048, H16), "e2": (2048, H16), "bcb": (2048, B16), "bc": (2048, H16),
-    "rexp": (2048, B16), "lb0": (1024, B16), "lb1": (1024, B16), "lb2": (1024, B16), "rvkb": (512, B16), "rvk": (512, H16),
-    "cmp": (2048, B16), "lg": (4096, B16), "mn": (4096, B16), "sb0": (1280, I32), "sb1": (1280, I32), "sb2": (1280, I32),
-    "ar0": (256, I32), "ar1": (256, I32), "ar2": (256, I32), "df": (2048, F32), "ab": (2048, F32), "rl": (2048, B16),
-    "eq": (4096, B16),
+    "em": (2048, B16), "ep": (2048, B16), "e1": (2048, B16), "e2": (2048, B16), "bc": (2048, B16), "rexp": (2048, B16),
+    "lb0": (1024, B16), "lb1": (1024, B16), "lb2": (1024, B16), "rvk": (512, B16), "cmp": (2048, B16), "lg": (4096, B16),
+    "mn": (4096, B16), "sb0": (1280, I32), "sb1": (1280, I32), "sb2": (1280, I32), "ar0": (256, I32), "ar1": (256, I32),
+    "ar2": (256, I32), "df": (2048, F32), "ab": (2048, F32), "rl": (2048, B16), "eq": (4096, B16),
 }
 SMALL = {
-    F32: "pcol 1 cols 16 rr0 128 rr1 128 rr2 128 cw0 8 cw1 8 cw2 8 kscan 256 m80 80 sel15 128 iow 16 iow1 16 xio 16 tm 16 kr 256 "
-         "mc 128 dumpc 16 cneg 8 totu 1 bad4 16 cc 256 sgc 256 ff 256 km 256 ma 256 mb 256 lo 256 t1 256 tt 256 own2 16 inc 80 "
-         "rk 80 q2 256 cq 256 chp 256 pk 256 fs 256 fg 256 ft 256 aa 256 aam 256 st1 16 st2 32 st4 64 mz 128 k1 128 k2 128 "
-         "k3 128 k4 64 k5 32 inv 16 keyw 16 cs 256 cn 256 tg 256 tn 256 es 256 ls 16 ls2 16 fo 16",
+    F32: "pcol 1 cols 16 rr0 128 rr1 128 rr2 128 cw0 8 cw1 8 cw2 8 kscan 256 m64 64 sel15 128 iow 16 iow1 16 iow4 16 xio 16 tm 16 "
+         "kr 256 mc 128 dumpc 16 cneg 8 totu 1 bad4 16 cc 256 sgc 256 ff 256 km 256 ma 256 mb 256 lo 256 t1 256 tt 256 own2 16 "
+         "inc 64 rk 64 chp 256 pk 256 fs 256 fg 256 ft 256 aa 256 aam 256 st1 16 st2 32 st4 64 mz 128 k1 128 k2 128 k3 128 k4 64 "
+         "k5 32 inv 16 keyw 16 cs 256 cn 256 tg 256 tn 256 es 256 ls 16 ls2 16 fo 16",
     B16: "blk 128 blk592 8 idb 128 shu 128 shd 128 cor 128 tmpb 128 mid 128 gum 128 gdm 128 ns0 128 ns1 128 ns2 128 ni0 128 "
          "ni1 128 ni2 128 t10 128 t11 128 t12 128 t20 128 t21 128 t22 128 r00 256 r01 256 r02 256 negb 256 io0 256 io1 256 "
-         "a1 128 m128 128 trb 128 orow 80 zb 256 live 128 w 128 wz 128 val 256 abc 256 ct 256 sd 256 st_ 256 oh 80 fa 256 "
+         "a1 128 m128 128 trb 128 orow 64 zb 256 w12 16 live 128 w 128 wz 128 val 256 abc 256 ct 256 sd 256 st_ 256 oh 64 fa 256 "
          "ent 256 dm 256 lsb 256",
-    H16: "id16 128 gu16 128 gd16 128 w12 16 nx 16 nt 16 d16 256 vk16 32 t32 128 ch16 256 mk 80 a16 256 key16 16 kb16 256",
+    H16: "nx 16 nt 16 d16 256 vk16 32 t32 128 ch16 256 mk 64 bo 16 a16 256 key16 16 kb16 256",
     I32: "icol 1 icol2 1 ti 256 ci 256 fi 256 ui 32 ui2 32 pi 16 h16 16 h16t 16 si 16 vk 32 vo 16 vo2 16 own 16 npi 256 "
          "npa 256 ai 256 ac 256 z 128 zi2 128 kmi 16 plc 16 oi 256 oc 256",
     U16: "pl 16 du 256 sl 16 zu 128 plu 16 fou 16",
@@ -204,11 +203,16 @@ def rank_program(g, core, T, topo):
     ts(col(2), col(1), 15.0, O.mult, 1.0, O.add)
     ts(col(3), col(1), -1000.0, O.mult)
     ts(col(4), col(1), 999.0, O.mult, 1.0, O.add)
-    fill(A("ones", 256, 2048), 1.0)
+    ts(col(5), col(0), 13.0, O.mult, 5.0, O.add)
+    ts(col(6), col(0), -14.0, O.mult, 255.0, O.add)
+    fill(A("negb"), -1.0)
+    ts(col(7), col(0), -1.0, O.mult, -2033.0, O.add)
+    ts(col(8), col(7), 8192.0, O.mult, 8192.0, O.add)
+    ts(col(9), col(1), -8192.0, O.mult)
+    ts(col(10), col(0), 0.0, O.is_equal, 8192.0, O.mult)
     for r in range(16):
         act(A("em", 128 * r + r, 128 * r + 128, 16), A("blk", 0, 128, 16), F.Copy)
     act(A("ep"), A("em"), F.Identity, scale=col(2))
-    fill(A("negb"), -1.0)
     sel(A("idb"), one(128), [[-1, 128]], O.is_equal, 0.0, 0, 1)
     sel(A("shu"), one(128), [[-1, 128]], O.is_equal, 0.0, -1, 1)
     sel(A("cor"), one(128), [[-1, 128]], O.is_equal, 0.0, 127, 1)
@@ -226,66 +230,63 @@ def rank_program(g, core, T, topo):
             tt(A("tmpb"), A("tmpb"), A("cor"), O.subtract)
             ts(A("mid"), A("idb"), -1.0, O.mult)
     act(A("cab", 2048, 2064), A("cab", 0, 16), F.Copy)
+    act(A("e1"), A("em"), F.Identity, scale=col(5))
+    act(A("e2"), A("em"), F.Identity, scale=col(6))
 
-    def round_constants(t):
-        start = STEP * (t + 1)
-        m0 = start // 16
-        ml = m0 - 1
-        sel(A("ns%d" % t), A("tmpb"), [[1, 128]], O.not_equal, 0.0, -ml, 0)
-        sel(A("ni%d" % t), A("mid"), [[1, 128]], O.not_equal, 0.0, -ml, 0)
+    def chunk(t):
+        m0 = STEP * (t + 1) // 16
+        return m0, m0 - 1
+
+    def round_g(t):
+        m0, ml = chunk(t)
         rr = "rr%d" % t
         iota(A(rr, 0, ml), [[1, ml]], 128, 0)
         iota(A(rr, m0, 128), [[1, 128 - m0]], m0, 0)
         iota(A(rr, ml, m0), [[0, 1]], 126, 0)
+        sel(A("cw%d" % t), one(8), [[0, 8]], O.not_equal, -128.0, -ml, 1)
+        sel(A("t2%d" % t), one(128), [[200, 128]], O.is_equal, 0.0, -127 - 200 * ml, 1)
+        sel(A("ns%d" % t), A("tmpb"), [[1, 128]], O.not_equal, 0.0, -ml, 0)
+        sel(A("ni%d" % t), A("mid"), [[1, 128]], O.not_equal, 0.0, -ml, 0)
+        sel(A("r0%d" % t), A("negb"), [[0, 256]], O.is_equal, 0.0, -m0, 1)
+        if t:
+            iota(A("lb%d" % t), [[0, 1024]], 0, 0)
+
+    def round_v(t):
+        m0, ml = chunk(t)
         ts(col(11), A("pcol"), float(m0), O.is_lt, 128.0, O.mult)
         tt(col(12), col(11), A("pcol"), O.add)
-        ts(A("t1%d" % t), A(rr), col(12), O.is_ge)
-        sel(A("t2%d" % t), one(128), [[200, 128]], O.is_equal, 0.0, -127 - 200 * ml, 1)
-        sel(A("r0%d" % t), A("negb"), [[0, 256]], O.is_equal, 0.0, -m0, 1)
-        fill(A("lb%d" % t), 0.0)
-        sel(A("cw%d" % t), one(8), [[0, 8]], O.not_equal, -128.0, -ml, 1)
+        ts(A("t1%d" % t), A("rr%d" % t), col(12), O.is_ge)
+        if t == 0:
+            fill(A("lb%d" % t), 0.0)
         cp(A("lb%d" % t, 15, 1024, 144), A("cw%d" % t))
 
-    round_constants(0)
-    ts(A("sel15"), A("blk"), col(1), O.mult)
+    round_g(0)
     iota(A("iow"), [[16, 16]], 0, 0)
-    ts(A("iow"), A("iow"), col(0), O.add)
-    ts(A("iow1"), A("iow"), 1.0, O.add)
-    cp(A("id16"), A("idb"))
+    round_v(0)
+    fill(A("ones", 256, 2048), 1.0)
 
     def rest_g():
-        sel(A("kscan"), one(256), [[0, 16], [1, 16]], O.not_equal, -4.0e6, 0, 0)
-        sel(A("shd"), one(128), [[-1, 128]], O.is_equal, 0.0, 1, 1)
-        sel(A("rvkb"), one(512), [[-8, 4], [-1, 8], [0, 16]], O.is_equal, 0.0, 0, 1)
-        sel(A("trb"), A("blk"), [[-1, 128]], O.is_ge, 0.0, 0, 1)
-        iota(A("mc"), [[2048, 8], [0, 16]], 0, 0)
-        iota(A("orow"), [[256, 5], [0, 16]], 0, 0)
-        sel(A("m80"), one(80), [[0, 5], [1, 16]], O.not_equal, 0.0, 0, 0)
         sel(A("rexp"), one(2048), [[-1, 128], [0, 16]], O.is_equal, 0.0, 0, 1)
-        sel(A("bcb"), one(2048), [[-1, 16], [-16, 8], [0, 16]], O.is_equal, 0.0, 0, 1)
+        sel(A("shd"), one(128), [[-1, 128]], O.is_equal, 0.0, 1, 1)
+        sel(A("trb"), A("blk"), [[-1, 128]], O.is_ge, 0.0, 0, 1)
+        sel(A("kscan"), one(256), [[0, 16], [1, 16]], O.not_equal, -4.0e6, 0, 0)
+        sel(A("rvk"), one(512), [[-8, 4], [-1, 8], [0, 16]], O.is_equal, 0.0, 0, 1)
+        iota(A("orow"), [[256, 4], [0, 16]], 0, 0)
+        sel(A("m64"), one(64), [[0, 4], [1, 16]], O.not_equal, 0.0, 0, 0)
 
     def rest_v():
-        ts(col(5), col(0), 13.0, O.mult, 5.0, O.add)
-        ts(col(6), col(0), -14.0, O.mult, 255.0, O.add)
-        ts(col(7), col(0), -1.0, O.mult, -2033.0, O.add)
-        ts(col(8), col(7), 8192.0, O.mult, 8192.0, O.add)
-        ts(col(9), col(1), -8192.0, O.mult)
-        ts(col(10), col(0), 0.0, O.is_equal, 8192.0, O.mult)
-        fill(A("zb"), 0.0)
         ts(A("blk592"), A("blk", 0, 128, 16), 592.0, O.mult)
         ts(A("w12", 0, 8), A("blk", 0, 128, 16), col(5), O.mult)
         ts(A("w12", 8, 16), A("blk", 0, 128, 16), col(6), O.mult)
+        fill(A("zb"), 0.0)
+        ts(A("iow4"), A("iow"), 0.25, O.mult, 256.0, O.add)
+        ts(A("dumpc"), A("iow"), float(DUMP), O.add)
+
+    def rest_v2():
         tt(A("gum"), A("idb"), A("shu"), O.subtract)
         tt(A("gdm"), A("idb"), A("shd"), O.subtract)
-        tt(A("gu16"), A("gum"), A("a1"), O.mult)
-        tt(A("gd16"), A("gdm"), A("m128"), O.mult)
-        ts(A("trb"), A("trb"), -1.0, O.mult)
-
-    def late_constants():
-        cp(A("bc"), A("bcb"))
-        iota(A("xio"), [[1, 16]], 0, 0)
-        ts(A("tm"), A("xio"), col(0), O.is_le, 0.5, O.mult)
-        ts(A("dumpc"), A("iow"), float(DUMP), O.add)
+        tt(A("gum"), A("gum"), A("a1"), O.mult)
+        tt(A("gdm"), A("gdm"), A("m128"), O.mult)
 
     def whash(src):
         for e in range(2):
@@ -314,20 +315,23 @@ def rank_program(g, core, T, topo):
         for u in range(16):
             mm(P(0, u, 128, 16), A("cab", off + u, off + u + 2033, 16), A("blk", 0, 128, 16))
         mm(P(3, 0, 256), A("a1", 0, 128, 1, 0, 1), A("io1", 0, 256, 1, 0, 1), True, False)
-        if t == 0:
-            ts(A("tab", 0, 512), A("detb", 0, 512), float(K), O.subtract)
         ts(A("live"), P(0, 0, 128), 0.5, O.is_gt)
         scan(A("w"), A("m128"), A("live"), O.mult, O.add)
         if t == 0:
-            for c in range(1, 4):
+            ts(A("sel15"), A("blk"), col(1), O.mult)
+            ts(A("iow"), A("iow"), col(0), O.add)
+            ts(A("iow1"), A("iow"), 1.0, O.add)
+            for c in range(4):
                 ts(A("tab", 512 * c, 512 * c + 512), A("detb", 512 * c, 512 * c + 512), float(K), O.subtract)
         mm(P(1, 0, 8), A("t1%d" % t), A("w", 15, 128, 16), True, False)
         mm(P(1, 0, 8), A("t2%d" % t), A("w", 15 - off, 128, 16), False, True)
+        mm(P(5, 0, 1), A("w"), A("ones", 0, 1))
         mm(P(2, 128, 136), A("ni%d" % t), A("w", 15, 128, 16))
         mm(P(2, 0, 128), A("ns%d" % t), A("w"))
         sel(A("wz"), A("w"), [[0, 8], [1, 16]], O.not_equal, 0.0, -15, 0)
         if t == 0:
             rest_g()
+        iota(A("sb%d" % t, 0, 1024), [[0, 1024]], K + 128, 0)
         act(A("cneg"), P(2, 128, 136), F.Copy)
         lb = "lb%d" % t
         for h in range(8):
@@ -335,26 +339,20 @@ def rank_program(g, core, T, topo):
             act(A(lb, 144 * h, 144 * h + 15), P(2, 16 * h, 16 * h + 15), F.Identity, bias=A("cneg", h, h + 1))
             if h == 3:
                 mm(P(3, 0, 256), A("wz"), A("r0%d" % t), False, False)
+            if h == 4:
+                act(A("totu"), P(5, 0, 1), F.Copy)
+                mm(P(5, 1, 2), A("sel15"), A("totu"))
             mm(P(3, 0, 256), A(lb, 128 * h, 128 * h + 128), A("cmp", 256 * h, 256 * h + 256), False, h == 7)
-        if t == 0:
-            rest_v()
-            fill(A("tab", 2048, TW), 128.0 - K)
-            fill(A("cab", 2064, TW), 0.0)
-            for c in range(4):
-                s = 512 * c
-                mm(P(4 + c, 0, 512), A("blk"), A("cab", s, s + 512))
-                act(P(4 + c, 0, 512), P(4 + c, 0, 512), F.Sign, bias=-0.5)
-                tt(A("tab", s, s + 512), A("tab", s, s + 512), P(4 + c, 0, 512), O.mult)
-        ts(A("val"), P(3, 0, 256), col(3), O.max, col(4), O.min)
-        mm(P(5, 0, 1), A("w"), A("ones", 0, 1))
-        act(A("totu"), P(5, 0, 1), F.Copy)
-        mm(P(5, 1, 2), A("sel15"), A("totu"))
         ts(A("nx"), A("iow1"), P(5, 1, 2), O.subtract, 0.0, O.max)
         ts(A("nt"), A("iow"), P(5, 1, 2), O.is_ge, float(DUMMY - start), O.mult)
-        fill(A("sb%d" % t, 0, 1024), float(K + 128))
-        mm(P(4, 0, 16), A("id16"), A("nx"), True, False)
-        mm(P(4, 0, 16), A("id16"), A("nt"), False, False)
+        mm(P(4, 0, 16), A("idb"), A("nx"), True, False)
+        mm(P(4, 0, 16), A("idb"), A("nt"), False, False)
+        ts(A("val"), P(3, 0, 256), col(3), O.max, col(4), O.min)
         wsum(P(4, 0, 16), "ep", "val", 0, 256, False)
+        if t == 0:
+            rest_v()
+            act(A("tab", 2048, TW), A("ones", 0, TW - 2048), F.Identity, bias=128.0 - K, scale=0.0)
+            act(A("cab", 2064, TW), A("ones", 0, TW - 2064), F.Identity, scale=0.0)
         ts(A("pl"), P(4, 0, 16), float(16 * m0 + off), O.add)
         ts(A("du"), ind(A("tab"), A("pl")), 1.0 / 256, O.mult, K / 256 - 0.5, O.add)
         act(A("abc"), ind(A("cab"), A("pl")), F.Copy)
@@ -364,7 +362,8 @@ def rank_program(g, core, T, topo):
             act(A("lg", 16 * a, 16 * b), ind(A("hamb"), A("du", a, b)), F.Copy)
         ts(A("d16"), A("du"), 2048.0, O.subtract)
         cp(A("ct"), P(7, 0, 256))
-        cp(A("ti"), ind(A("tab"), A("pl")))
+        if t == 0:
+            rest_v2()
         for h in range(2):
             for e in range(2):
                 mm(P(4, 16 * e + 8 * h, 16 * e + 8 * h + 8), A("d16", 128 * h, 128 * h + 128), A("w12", 8 * e, 8 * e + 8))
@@ -374,13 +373,14 @@ def rank_program(g, core, T, topo):
 
         for b in range(4):
             rep(b)
-        mm(P(7, 0, 256), A("gu16"), A("d16"))
-        mm(P(7, 256, 512), A("gd16"), A("d16"))
+        mm(P(7, 0, 256), A("gum"), A("d16"))
+        mm(P(7, 256, 512), A("gdm"), A("d16"))
         cp(A("ui"), P(4, 0, 32))
         ts(A("ui2"), A("ui"), 4095, O.bitwise_and)
         tt(A("pi"), A("ui2", 0, 16), A("ui2", 16, 32), O.mult)
         ts(A("h16"), A("pi"), 1, O.arith_shift_right, 0x7FFFFFF0, O.bitwise_and)
         ts(A("h16t"), A("h16"), float(16 * t), O.add)
+        cp(A("lg", 3584, 4096), ind(A("hamb"), A("du", 224, 256)))
         for b in range(8):
             s = 512 * b
             tt(A("mn", s, s + 512), A("lg", s, s + 512), P(b % 4, 0, 512), O.min)
@@ -391,38 +391,31 @@ def rank_program(g, core, T, topo):
                 for k in range(16):
                     mm(P(6, 128 * h + k, 128 * h + 128, 16), A("mn", 2048 * h + k, 2048 * h + 2048, 16), A("blk592"))
         if t == 0:
-            ts(A("e1"), A("em"), col(5), O.mult)
-            ts(A("e2"), A("em"), col(6), O.mult)
-            cp(A("rvk"), A("rvkb"))
             ts(A("rvk", 0, 256), A("rvk", 0, 256), -1.0, O.mult)
+            ts(A("trb"), A("trb"), -1.0, O.mult)
+        cp(A("ti"), ind(A("tab"), A("pl")))
         ts(A("fi"), A("ti"), 255, O.bitwise_and, 2, O.arith_shift_right)
         ts(A("ff"), A("fi"), 32.0, O.subtract)
-        ts(A("ci"), A("ti"), 255, O.bitwise_and)
-        ts(A("cc"), A("ci"), 128.0, O.subtract)
-        act(A("sgc"), A("cc"), F.Sign)
-        act(A("fa"), A("abc"), F.Relu, bias=-1.0)
-        mm(P(3, 0, 256), A("blk"), A("fa"))
-        act(A("fs"), P(3, 0, 256), F.Sign, bias=-0.5)
-        mm(P(5, 0, 256), A("id16"), A("d16"))
+        act(P(7, 0, 256), P(7, 0, 256), F.Identity, bias=col(9))
+        act(P(7, 256, 512), P(7, 256, 512), F.Identity, bias=col(10))
+        mm(P(5, 0, 256), A("idb"), A("d16"))
         scan(A("km"), A("kscan"), P(6, 0, 256), O.add, O.max)
         tt(A("si"), A("km", 15, 256, 16), A("h16t"), O.add)
         ts(A("vk", 0, 16), A("si"), 4, O.arith_shift_right, 4095, O.bitwise_and)
         ts(A("vk", 16, 32), A("si"), 15, O.bitwise_and)
         ts(A("vk16"), A("vk"), 2048.0, O.subtract)
-        mm(P(4, 0, 128, 1, 0, 32), A("vk16"), A("id16"))
+        mm(P(4, 0, 128, 1, 0, 32), A("vk16"), A("idb"))
         cp(A("t32", 0, 128, 1, 0, 32), P(4, 0, 128, 1, 0, 32))
-        ts(P(7, 0, 256), P(7, 0, 256), col(9), O.add)
-        ts(P(7, 256, 512), P(7, 256, 512), col(10), O.add)
         for h in range(2):
             s = 128 * h
             mm(P(1, s, s + 128), A("rvk", 256 + s, 256 + s + 128, 1, 0, 32), A("t32", 0, 128, 1, 0, 32))
         for h in range(2):
             s = 128 * h
-            mm(P(0, s, s + 128), A("id16"), A("d16", s, s + 128), True, False)
+            mm(P(0, s, s + 128), A("idb"), A("d16", s, s + 128), True, False)
             mm(P(0, s, s + 128), A("rvk", s, s + 128, 1, 0, 32), A("t32", 0, 128, 1, 0, 32), False, True)
         ts(A("ma"), P(1, 0, 256), col(7), O.is_ge)
-        act(A("mb"), P(1, 0, 256), F.Relu, bias=col(8), scale=-8192.0)
         act(A("sd"), P(0, 0, 256), F.Sign)
+        act(A("mb"), P(1, 0, 256), F.Relu, bias=col(8), scale=-8192.0)
         wsum(P(3, 0, 16), "em", "sd", 0, 256)
         tt(P(2, 0, 256), P(7, 0, 256), A("ma"), O.mult)
         tt(A("lo"), P(7, 256, 512), A("mb"), O.min)
@@ -432,29 +425,34 @@ def rank_program(g, core, T, topo):
         act(A("st_"), A("tt"), F.Sign)
         mm(P(5, 256, 512), A("blk"), A("st_"))
         whash("ch16")
+        act(A("fa"), A("abc"), F.Relu, bias=-1.0)
+        mm(P(2, 0, 256), A("blk"), A("fa"))
+        act(A("fs"), P(2, 0, 256), F.Sign, bias=-0.5)
         cp(A("vo"), P(3, 0, 16))
         ts(A("vo2"), A("vo"), 1, O.bitwise_and)
         tt(A("bad4"), A("vo2"), A("nt"), O.max)
         ts(A("bad4"), A("bad4"), 0.0, O.is_gt, 4.0, O.mult)
+        tt(A("bo"), A("bad4"), A("iow4"), O.mult)
         ts(A("chp"), A("ch16"), 256.0, O.mult, 2048.0 * 256 + 128, O.add)
         cp(A("npi"), P(5, 256, 512))
         ts(A("npa"), A("npi"), 1, O.bitwise_and)
-        ts(A("q2"), A("npa"), 2.0, O.mult, -1.0, O.add)
-        tt(A("cq"), A("q2"), A("ff"), O.mult)
-        tt(A("pk"), A("chp"), A("cq"), O.add)
+        ts(P(1, 0, 256), A("npa"), 2.0, O.mult, -1.0, O.add)
+        tt(P(1, 0, 256), P(1, 0, 256), A("ff"), O.mult)
+        tt(A("pk"), P(1, 0, 256), A("chp"), O.add)
         mix()
         ts(A("own"), A("pi"), 5, O.arith_shift_right, 3, O.bitwise_and)
         tt(A("own2"), A("own"), A("bad4"), O.max)
-        for o in range(5):
+        for o in range(4):
             ts(A("oh", 16 * o, 16 * o + 16), A("own2"), float(o), O.is_equal)
-        mm(P(7, 80, 160), A("blk"), A("oh"))
-        mm(P(4, 0, 80), A("ones", 0, 128, 1, 0, 1), A("orow", 0, 80, 1, 0, 1), True, False)
-        mm(P(4, 0, 80), A("trb"), A("oh"), False, True)
-        scan(A("inc"), A("m80"), P(7, 80, 160), O.mult, O.add)
-        tt(A("rk"), A("inc"), P(4, 0, 80), O.add)
+        mm(P(7, 64, 128), A("blk"), A("oh"))
+        mm(P(4, 0, 64), A("ones", 0, 128, 1, 0, 1), A("orow", 0, 64, 1, 0, 1), True, False)
+        mm(P(4, 0, 64), A("trb"), A("oh"), False, True)
+        scan(A("inc"), A("m64"), P(7, 64, 128), O.mult, O.add)
+        tt(A("rk"), A("inc"), P(4, 0, 64), O.add)
         tt(A("mk"), A("rk"), A("oh"), O.mult)
-        for o in range(5):
-            mm(P(3, 0, 16), A("id16"), A("mk", 16 * o, 16 * o + 16), o == 0, o == 4)
+        mm(P(3, 0, 16), A("idb"), A("bo"), True, False)
+        for o in range(4):
+            mm(P(3, 0, 16), A("idb"), A("mk", 16 * o, 16 * o + 16), False, o == 3)
         cp(A("sl"), P(3, 0, 16))
         sb, ar, arr = "sb%d" % t, "ar%d" % t, "arr%d" % t
         cp(ind(A(sb), A("sl")), A("pk"))
@@ -466,13 +464,29 @@ def rank_program(g, core, T, topo):
         need("g", [], [A(sb)])
         g.remote_dma_fused(trs, local_sem=T.sem.sent)
         got = sum(len(es) for q in range(N) if q != rank for o, es in plan(topo, T.cores, q) if o == rank)
+        if t == 0:
+            sel(A("bc"), one(2048), [[-1, 16], [-16, 8], [0, 16]], O.is_equal, 0.0, 0, 1)
+            iota(A("mc"), [[2048, 8], [0, 16]], 0, 0)
+            iota(A("xio"), [[1, 16]], 0, 0)
+        if not last:
+            round_g(t + 1)
         cp(A(ar, 64 * rank, 64 * rank + 64), A(sb, 256 * rank, 256 * rank + 64))
+        ts(A("ci"), A("ti"), 255, O.bitwise_and)
+        ts(A("cc"), A("ci"), 128.0, O.subtract)
+        act(A("sgc"), A("cc"), F.Sign)
+        if t == 0:
+            for c in range(4):
+                s = 512 * c
+                mm(P(c % 3, 0, 512), A("blk"), A("cab", s, s + 512))
+                act(P(c % 3, 0, 512), P(c % 3, 0, 512), F.Sign, bias=-0.5)
+                tt(A("tab", s, s + 512), A("tab", s, s + 512), P(c % 3, 0, 512), O.mult)
+        if not last:
+            cp(ind(A("cab"), A("pl")), A("fa"))
         tt(A("fg"), A("ti"), A("sgc"), O.subtract)
         tt(A("ft"), A("fg"), A("fs"), O.mult)
         cp(ind(A("tab"), A("pl")), A("ft"))
         if not last:
-            cp(ind(A("cab"), A("pl")), A("fa"))
-            fill(A("tab", 2048, DUMP), 128.0 - K)
+            iota(A("tab", 2048, DUMP), [[0, DUMP - 2048]], 128 - K, 0)
         ts(A("ai"), A(ar), 8, O.arith_shift_right, extra=[(arr, got)])
         ts(A("a16"), A("ai"), 2048.0, O.subtract)
         whash("a16")
@@ -482,14 +496,17 @@ def rank_program(g, core, T, topo):
         mix(True)
         ts(A("z", 0, 16), A("pi"), 7, O.arith_shift_right, 2047, O.bitwise_and)
         tt(A("z", 16, 32), A("z", 0, 16), A("st1"), O.add)
-        tt(A("z", 32, 64), A("z", 0, 32), A("st2"), O.add)
-        tt(A("z", 64, 128), A("z", 0, 64), A("st4"), O.add)
-        ts(A("zi2"), A("z"), 2047, O.bitwise_and)
-        cp(A("zu"), A("zi2"))
+        ts(A("zi2", 0, 32), A("z", 0, 32), 2047, O.bitwise_and)
+        cp(A("zu", 0, 32), A("zi2", 0, 32))
         late = []
         for m in range(8):
             s = 256 * m
             tt(A("df", s, s + 256), ind(A("tab"), A("zu", 16 * m, 16 * m + 16)), A("aa"), O.subtract)
+            if m == 0:
+                tt(A("z", 32, 64), A("z", 0, 32), A("st2"), O.add)
+                tt(A("z", 64, 128), A("z", 0, 64), A("st4"), O.add)
+                ts(A("zi2", 32, 128), A("z", 32, 128), 2047, O.bitwise_and)
+                cp(A("zu", 32, 128), A("zi2", 32, 128))
             act(A("ab", s, s + 256), A("df", s, s + 256), F.Abs)
             while late:
                 z = late.pop()
@@ -502,7 +519,9 @@ def rank_program(g, core, T, topo):
                 wsum(P(m // 4, 0, 64), "em", "rl", 256 * m - 768, 256 * m + 256)
         tt(A("mz"), A("mc"), A("zi2"), O.add)
         if t == 0:
-            late_constants()
+            ts(A("tm"), A("xio"), col(0), O.is_le, 0.5, O.mult)
+        if not last:
+            round_v(t + 1)
         for h in range(2):
             a, b = 64 * h, 64 * h + 64
             ts(A("k1", a, b), P(h, 0, 64), 0.5, O.is_gt, 32768.0, O.mult)
@@ -530,19 +549,16 @@ def rank_program(g, core, T, topo):
             ts(e, A("kb16", 16 * c + 16, 256), A("keyw", c, c + 1), O.is_equal)
             mm(P(3, 16 * c + 16, 256), A("blk"), e, False, False)
             if c == 13:
-                tt(A("dm"), A("kr"), A("kb16"), O.is_equal)
+                tt(A("dm"), P(2, 0, 256), A("kr"), O.is_equal)
         mm(P(3, 0, 256), A("blk"), A("dm"), False, True)
-        tt(A("cs"), A("oc"), A("ac"), O.add)
         act(A("lsb"), P(3, 0, 256), F.Copy)
+        tt(A("cs"), A("oc"), A("ac"), O.add)
         ts(A("cn"), A("cs"), 129.0, O.max, 383.0, O.min)
         act(A("ent"), A("cn"), F.Abs, bias=-256.0)
-        mm(P(5, 0, 256), A("blk"), A("ent"))
         wsum(P(4, 0, 16), "em", "lsb", 0, 256)
         tt(A("tg"), A("aam"), A("cn"), O.add)
+        mm(P(5, 0, 256), A("blk"), A("ent"))
         act(A("es"), P(5, 0, 256), F.Sign, bias=-0.5)
-        tt(A("tn"), A("tg"), A("es"), O.mult)
-        if not last:
-            round_constants(t + 1)
         tt(A("ls"), A("inv"), P(4, 0, 16), O.subtract)
         ts(A("ls2"), A("ls"), -0.5, O.is_lt)
         tt(A("ls"), A("ls2"), A("dumpc"), O.mult)
@@ -551,6 +567,7 @@ def rank_program(g, core, T, topo):
         if not last:
             cp(ind(A("cab"), A("fou")), A("ent"))
             cp(A("cab", 2048, 2064), A("cab", 0, 16))
+        tt(A("tn"), A("tg"), A("es"), O.mult)
         cp(ind(A("tab"), A("fou")), A("tn"))
 
     for c in range(4):

from concourse.bass import DstId, RemoteDMATransfer
from concourse.mybir import AluOpType as O, ActivationFunctionType as F

RO, STEP, N, CAP = 3, 650, 4, 64
CH = ((0, 64), (64, 128), (128, 192), (192, 224))
TW = 2576
DUMMY, DUMP = 2064, 2320
K = 1 << 22
F32, B16, H16, I32, U16 = "float32", "bfloat16", "float16", "int32", "uint16"

WIDE = {
    "detb": (2048, I32), "big": (2048, I32), "tab": (TW, F32), "cab": (TW, B16), "hamb": (4096, B16), "ones": (2048, B16),
    "em": (2048, B16), "ep": (2048, B16), "e1": (2048, B16), "e2": (2048, B16), "bc": (2048, B16), "rexp": (2048, B16),
    "lb0": (1024, B16), "lb1": (1024, B16), "lb2": (1024, B16), "rvk": (512, B16), "cmp": (2048, B16), "lg": (4096, B16),
    "mn": (4096, B16), "sb0": (1280, I32), "sb1": (1280, I32), "sb2": (1280, I32), "ar0": (256, I32), "ar1": (256, I32),
    "ar2": (256, I32), "df": (2048, F32), "ab": (2048, F32), "rl": (2048, B16), "eq": (4096, B16),
}
SMALL = {
    F32: "pcol 1 cols 16 rr0 128 rr1 128 rr2 128 cw0 8 cw1 8 cw2 8 kscan 256 m64 64 sel15 128 iow 16 iow1 16 iow4 16 xio 16 tm 16 "
         "kr 256 mc 128 dumpc 16 cneg 8 totu 1 bad4 16 cc 256 sgc 256 ff 256 km 256 ma 256 mb 256 lo 256 t1 256 tt 256 own2 16 "
         "inc 64 rk 64 chp 256 pk 256 fs 256 fg 256 ft 256 aa 256 aam 256 st1 16 st2 32 st4 64 mz 128 k1 128 k2 128 k3 128 k4 64 "
         "k5 32 inv 16 keyw 16 cs 256 cn 256 tg 256 tn 256 es 256 ls 16 ls2 16 fo 16",
    B16: "blk 128 blk592 8 idb 128 shu 128 shd 128 cor 128 tmpb 128 mid 128 gum 128 gdm 128 ns0 128 ns1 128 ns2 128 ni0 128 "
         "ni1 128 ni2 128 t10 128 t11 128 t12 128 t20 128 t21 128 t22 128 r00 256 r01 256 r02 256 negb 256 io0 256 io1 256 "
         "a1 128 m128 128 trb 128 orow 64 zb 256 w12 16 live 128 w 128 wz 128 val 256 abc 256 ct 256 sd 256 st_ 256 oh 64 fa 256 "
         "ent 256 dm 256 lsb 256",
    H16: "nx 16 nt 16 d16 256 vk16 32 t32 128 ch16 256 mk 64 bo 16 a16 256 key16 16 kb16 256",
    I32: "icol 1 icol2 1 ti 256 ci 256 fi 256 ui 32 ui2 32 pi 16 h16 16 h16t 16 si 16 vk 32 vo 16 vo2 16 own 16 npi 256 "
         "npa 256 ai 256 ac 256 z 128 zi2 128 kmi 16 plc 16 oi 256 oc 256",
    U16: "pl 16 du 256 sl 16 zu 128 plu 16 fou 16",
}


def _layout():
    scratch, place = {}, {}
    for i in range(8):
        scratch["p%d" % i] = ("psum", [128, 512], F32)
        place["p%d" % i] = ("p%d" % i, 0, 512)
    for name in WIDE:
        scratch[name] = ("sbuf", [128, WIDE[name][0]], WIDE[name][1])
        place[name] = (name, 0, WIDE[name][0])
    for dtype in SMALL:
        words = SMALL[dtype].split()
        at = 0
        for j in range(0, len(words), 2):
            w = int(words[j + 1])
            place[words[j]] = ("w_" + dtype, at, w)
            at += (w + 15) // 16 * 16
        scratch["w_" + dtype] = ("sbuf", [128, at], dtype)
    return scratch, place


SCRATCH, PLACE = _layout()
SEMAPHORES = ["sv", "ss", "st", "sg", "sent", "ldh"] + ["ld%d" % i for i in range(4)] + ["out%d" % i for i in range(4)] + ["arr%d" % i for i in range(RO)]
SEMOF = {"v": "sv", "s": "ss", "t": "st", "g": "sg"}


def plan(topo, cores, rank):
    a = topo.chip(cores[rank])

    def far(o):
        b = topo.chip(cores[o])
        return 0 if topo.mates(a, b) or topo.same_plane(a, b) else 1
    out, used = [], 0
    others = sorted([o for o in range(N) if o != rank], key=far)
    for o in others:
        n = 4 if o == others[-1] else 2
        out.append((o, topo.engines(cores[rank], cores[o])[used:used + n]))
        used += n
    return out


def rank_program(g, core, T, topo):
    rank = T.rank_of(core)
    if rank is None:
        return
    queues = {"v": g.vector, "s": g.scalar, "t": g.tensor, "g": g, "y": g.sync}
    count = {"v": 0, "s": 0, "t": 0, "g": 0}
    known = {q: {} for q in queues}
    clock, hist, srcq = {}, {}, {}

    def A(name, c0=0, c1=None, step=1, p0=0, p1=128):
        buf, base, w = PLACE[name]
        lo, hi = base + c0, base + (w if c1 is None else c1)
        t = T[buf]
        ap = t[p0:p1, lo:hi] if step == 1 else t[p0:p1, lo:hi:step]
        return (ap, buf, lo, hi)

    def P(b, c0, c1, step=1, p0=0, p1=128):
        return A("p%d" % b, c0, c1, step, p0, p1)

    def ind(win, off):
        return (win[0].indirect(off[0]), win, off)

    def flat(x):
        return [x[1], x[2]] if len(x) == 3 else [x]

    def ispsum(buf):
        return buf[0] == "p" and buf[1:].isdigit()

    def need(q, outs, ins, extra=()):
        want = dict(extra)
        acc = [(a, "w") for o in outs for a in flat(o)] + [(a, "r") for i in ins for a in flat(i)]
        for (_, buf, lo, hi), kind in acc:
            ps = ispsum(buf)
            for (sq, idx, k2, l2, h2) in hist.get(buf, ()):
                if sq == q == "t":
                    continue
                if (ps and sq != q) or ((kind == "w" or k2 == "w") and lo < h2 and l2 < hi):
                    want[sq] = max(want.get(sq, 0), idx)
        for s in sorted(want):
            if known[q].get(s, 0) < want[s]:
                queues[q].wait_ge(T.sem[SEMOF.get(s, s)], want[s])
                known[q][s] = want[s]
                for k, v in clock.get((s, want[s]), {}).items():
                    known[q][k] = max(known[q].get(k, 0), v)
        return acc

    def note(q, idx, acc):
        clock[(q, idx)] = dict(known[srcq.get(q, q)])
        for (_, buf, lo, hi), kind in acc:
            old = hist.get(buf, [])
            if ispsum(buf):
                keep = [e for e in old if e[0] == q and q != "t" and not (kind == "w" and lo <= e[3] and e[4] <= hi)]
            else:
                keep = [e for e in old if not (lo <= e[3] and e[4] <= hi and (kind == "w" or (e[2] == "r" and e[0] == q)))]
            hist[buf] = keep + [(q, idx, kind, lo, hi)]

    def emit(q, outs, ins, call, extra=()):
        acc = need(q, outs, ins, extra)
        r = call()
        count[q] += 1
        r.then_inc(T.sem[SEMOF[q]], 1)
        note(q, count[q], acc)

    def load(q, sem, out, src):
        acc = need(q, [out], [])
        queues[q].dma_start(out[0], src).then_inc(T.sem[sem], 16)
        srcq[sem] = q
        note(sem, 16, acc)

    def store(q, sem, dst, i):
        acc = need(q, [], [i])
        queues[q].dma_start(dst, i[0]).then_inc(T.sem[sem], 16)
        srcq[sem] = q
        note(sem, 16, acc)

    def mm(out, l, r, start=True, stop=True):
        emit("t", [out], [l, r], lambda: g.tensor.matmul(out[0], l[0], r[0], start, stop))

    def cp(out, i):
        emit("v", [out], [i], lambda: g.vector.tensor_copy(out[0], i[0]))

    def tt(out, a, b, op):
        emit("v", [out], [a, b], lambda: g.vector.tensor_tensor(out[0], a[0], b[0], op))

    def ts(out, i, s1, op0, s2=None, op1=None, extra=()):
        ins = [i] + [s for s in (s1, s2) if isinstance(s, tuple)]
        x1 = s1[0] if isinstance(s1, tuple) else s1
        x2 = s2[0] if isinstance(s2, tuple) else s2
        if op1 is None:
            emit("v", [out], ins, lambda: g.vector.tensor_scalar(out[0], i[0], x1, None, op0), extra)
        else:
            emit("v", [out], ins, lambda: g.vector.tensor_scalar(out[0], i[0], x1, x2, op0, op1), extra)

    def scan(out, a, b, op0, op1):
        emit("v", [out], [a, b], lambda: g.vector.tensor_tensor_scan(out[0], a[0], b[0], 0.0, op0, op1))

    def fill(out, c):
        emit("v", [out], [], lambda: g.vector.memset(out[0], c))

    def act(out, i, func, bias=0.0, scale=1.0):
        ins = [i] + [s for s in (bias, scale) if isinstance(s, tuple)]
        b = bias[0] if isinstance(bias, tuple) else bias
        c = scale[0] if isinstance(scale, tuple) else scale
        if func == F.Copy:
            emit("s", [out], ins, lambda: g.scalar.activation(out[0], i[0], func))
        else:
            emit("s", [out], ins, lambda: g.scalar.activation(out[0], i[0], func, bias=b, scale=c))

    def iota(out, pat, base, cm):
        emit("g", [out], [], lambda: g.iota(out[0], pat, base, cm, allow_small_or_imprecise_dtypes=True))

    def sel(out, i, pat, op, fillv, base, cm):
        emit("g", [out], [i], lambda: g.affine_select(out[0], i[0], pat, op, fillv, base, cm))

    one = lambda w: A("ones", 0, w)
    col = lambda j: A("cols", j, j + 1)

    for c in range(4):
        load("y", "ld%d" % c, A("detb", 512 * c, 512 * c + 512), T.det[:, 512 * c:512 * c + 512])
    load("s", "ldh", A("hamb"), T.ham[:, :])

    fill(A("ones", 0, 256), 1.0)
    fill(A("em"), 0.0)
    iota(A("icol"), [[0, 1]], 0, 1)
    sel(A("tmpb"), one(128), [[-16, 8], [0, 16]], O.is_ge, 0.0, 0, 1)
    sel(A("blk"), A("tmpb"), [[16, 8], [0, 16]], O.is_ge, 0.0, 15, -1)
    ts(A("icol2"), A("icol"), 15, O.bitwise_and)
    cp(A("pcol"), A("icol"))
    cp(col(0), A("icol2"))
    ts(col(1), col(0), 15.0, O.is_equal)
    ts(col(2), col(1), 15.0, O.mult, 1.0, O.add)
    ts(col(3), col(1), -1000.0, O.mult)
    ts(col(4), col(1), 999.0, O.mult, 1.0, O.add)
    ts(col(5), col(0), 13.0, O.mult, 5.0, O.add)
    ts(col(6), col(0), -14.0, O.mult, 255.0, O.add)
    fill(A("negb"), -1.0)
    ts(col(7), col(0), -1.0, O.mult, -2033.0, O.add)
    ts(col(8), col(7), 8192.0, O.mult, 8192.0, O.add)
    ts(col(9), col(1), -8192.0, O.mult)
    ts(col(10), col(0), 0.0, O.is_equal, 8192.0, O.mult)
    for r in range(16):
        act(A("em", 128 * r + r, 128 * r + 128, 16), A("blk", 0, 128, 16), F.Copy)
    act(A("ep"), A("em"), F.Identity, scale=col(2))
    sel(A("idb"), one(128), [[-1, 128]], O.is_equal, 0.0, 0, 1)
    sel(A("shu"), one(128), [[-1, 128]], O.is_equal, 0.0, -1, 1)
    sel(A("cor"), one(128), [[-1, 128]], O.is_equal, 0.0, 127, 1)
    sel(A("m128"), one(128), [[0, 8], [1, 16]], O.not_equal, 0.0, 0, 0)
    sel(A("a1"), one(128), [[0, 8], [1, 16]], O.not_equal, 0.0, -15, 0)
    iota(A("io0"), [[1, 256]], 0, 0)
    iota(A("io1"), [[1, 256]], 1, 0)
    for c in range(4):
        s = 512 * c
        ts(A("big", s, s + 512), A("detb", s, s + 512), 255, O.bitwise_and)
        ts(A("df", s, s + 512), A("big", s, s + 512), 128.0, O.subtract)
        act(A("cab", s, s + 512), A("df", s, s + 512), F.Abs)
        if c == 0:
            tt(A("tmpb"), A("idb"), A("shu"), O.subtract)
            tt(A("tmpb"), A("tmpb"), A("cor"), O.subtract)
            ts(A("mid"), A("idb"), -1.0, O.mult)
    act(A("cab", 2048, 2064), A("cab", 0, 16), F.Copy)
    act(A("e1"), A("em"), F.Identity, scale=col(5))
    act(A("e2"), A("em"), F.Identity, scale=col(6))

    def chunk(t):
        m0 = STEP * (t + 1) // 16
        return m0, m0 - 1

    def round_g(t):
        m0, ml = chunk(t)
        rr = "rr%d" % t
        iota(A(rr, 0, ml), [[1, ml]], 128, 0)
        iota(A(rr, m0, 128), [[1, 128 - m0]], m0, 0)
        iota(A(rr, ml, m0), [[0, 1]], 126, 0)
        sel(A("cw%d" % t), one(8), [[0, 8]], O.not_equal, -128.0, -ml, 1)
        sel(A("t2%d" % t), one(128), [[200, 128]], O.is_equal, 0.0, -127 - 200 * ml, 1)
        sel(A("ns%d" % t), A("tmpb"), [[1, 128]], O.not_equal, 0.0, -ml, 0)
        sel(A("ni%d" % t), A("mid"), [[1, 128]], O.not_equal, 0.0, -ml, 0)
        sel(A("r0%d" % t), A("negb"), [[0, 256]], O.is_equal, 0.0, -m0, 1)
        if t:
            iota(A("lb%d" % t), [[0, 1024]], 0, 0)

    def round_v(t):
        m0, ml = chunk(t)
        ts(col(11), A("pcol"), float(m0), O.is_lt, 128.0, O.mult)
        tt(col(12), col(11), A("pcol"), O.add)
        ts(A("t1%d" % t), A("rr%d" % t), col(12), O.is_ge)
        if t == 0:
            fill(A("lb%d" % t), 0.0)
        cp(A("lb%d" % t, 15, 1024, 144), A("cw%d" % t))

    round_g(0)
    iota(A("iow"), [[16, 16]], 0, 0)
    round_v(0)
    fill(A("ones", 256, 2048), 1.0)

    def rest_g():
        sel(A("rexp"), one(2048), [[-1, 128], [0, 16]], O.is_equal, 0.0, 0, 1)
        sel(A("shd"), one(128), [[-1, 128]], O.is_equal, 0.0, 1, 1)
        sel(A("trb"), A("blk"), [[-1, 128]], O.is_ge, 0.0, 0, 1)
        sel(A("kscan"), one(256), [[0, 16], [1, 16]], O.not_equal, -4.0e6, 0, 0)
        sel(A("rvk"), one(512), [[-8, 4], [-1, 8], [0, 16]], O.is_equal, 0.0, 0, 1)
        iota(A("orow"), [[256, 4], [0, 16]], 0, 0)
        sel(A("m64"), one(64), [[0, 4], [1, 16]], O.not_equal, 0.0, 0, 0)

    def rest_v():
        ts(A("blk592"), A("blk", 0, 128, 16), 592.0, O.mult)
        ts(A("w12", 0, 8), A("blk", 0, 128, 16), col(5), O.mult)
        ts(A("w12", 8, 16), A("blk", 0, 128, 16), col(6), O.mult)
        fill(A("zb"), 0.0)
        ts(A("iow4"), A("iow"), 0.25, O.mult, 256.0, O.add)
        ts(A("dumpc"), A("iow"), float(DUMP), O.add)

    def rest_v2():
        tt(A("gum"), A("idb"), A("shu"), O.subtract)
        tt(A("gdm"), A("idb"), A("shd"), O.subtract)
        tt(A("gum"), A("gum"), A("a1"), O.mult)
        tt(A("gdm"), A("gdm"), A("m128"), O.mult)

    def whash(src):
        for e in range(2):
            for r in range(16):
                mm(P(6, 16 * e, 16 * e + 16), A("e%d" % (e + 1), 128 * r, 128 * r + 128), A(src, r, 256, 16), r == 0, r == 15)

    def mix(steps=False):
        cp(A("ui"), P(6, 0, 32))
        ts(A("ui2"), A("ui"), 4095, O.bitwise_and)
        if steps:
            ts(A("st1"), A("ui2", 0, 16), 2.0, O.mult, 1.0, O.add)
            for j in range(2):
                act(A("st2", 16 * j, 16 * j + 16), A("st1"), F.Identity, scale=2.0)
            for j in range(2):
                act(A("st4", 32 * j, 32 * j + 32), A("st2"), F.Identity, scale=2.0)
        tt(A("pi"), A("ui2", 0, 16), A("ui2", 16, 32), O.mult)

    def wsum(out, weights, src, c0, c1, start=True):
        for r in range(16):
            mm(out, A(weights, 128 * r, 128 * r + 128), A(src, c0 + r, c1, 16), start and r == 0, r == 15)

    for t in range(RO):
        start = STEP * (t + 1)
        m0, off = start // 16, start % 16
        last = t == RO - 1
        for u in range(16):
            mm(P(0, u, 128, 16), A("cab", off + u, off + u + 2033, 16), A("blk", 0, 128, 16))
        mm(P(3, 0, 256), A("a1", 0, 128, 1, 0, 1), A("io1", 0, 256, 1, 0, 1), True, False)
        ts(A("live"), P(0, 0, 128), 0.5, O.is_gt)
        scan(A("w"), A("m128"), A("live"), O.mult, O.add)
        if t == 0:
            ts(A("sel15"), A("blk"), col(1), O.mult)
            ts(A("iow"), A("iow"), col(0), O.add)
            ts(A("iow1"), A("iow"), 1.0, O.add)
            for c in range(4):
                ts(A("tab", 512 * c, 512 * c + 512), A("detb", 512 * c, 512 * c + 512), float(K), O.subtract)
        mm(P(1, 0, 8), A("t1%d" % t), A("w", 15, 128, 16), True, False)
        mm(P(1, 0, 8), A("t2%d" % t), A("w", 15 - off, 128, 16), False, True)
        mm(P(5, 0, 1), A("w"), A("ones", 0, 1))
        mm(P(2, 128, 136), A("ni%d" % t), A("w", 15, 128, 16))
        mm(P(2, 0, 128), A("ns%d" % t), A("w"))
        sel(A("wz"), A("w"), [[0, 8], [1, 16]], O.not_equal, 0.0, -15, 0)
        if t == 0:
            rest_g()
        iota(A("sb%d" % t, 0, 1024), [[0, 1024]], K + 128, 0)
        act(A("cneg"), P(2, 128, 136), F.Copy)
        lb = "lb%d" % t
        for h in range(8):
            ts(A("cmp", 256 * h, 256 * h + 256), A("io0"), P(1, h, h + 1), O.is_ge)
            act(A(lb, 144 * h, 144 * h + 15), P(2, 16 * h, 16 * h + 15), F.Identity, bias=A("cneg", h, h + 1))
            if h == 3:
                mm(P(3, 0, 256), A("wz"), A("r0%d" % t), False, False)
            if h == 4:
                act(A("totu"), P(5, 0, 1), F.Copy)
                mm(P(5, 1, 2), A("sel15"), A("totu"))
            mm(P(3, 0, 256), A(lb, 128 * h, 128 * h + 128), A("cmp", 256 * h, 256 * h + 256), False, h == 7)
        ts(A("nx"), A("iow1"), P(5, 1, 2), O.subtract, 0.0, O.max)
        ts(A("nt"), A("iow"), P(5, 1, 2), O.is_ge, float(DUMMY - start), O.mult)
        mm(P(4, 0, 16), A("idb"), A("nx"), True, False)
        mm(P(4, 0, 16), A("idb"), A("nt"), False, False)
        ts(A("val"), P(3, 0, 256), col(3), O.max, col(4), O.min)
        wsum(P(4, 0, 16), "ep", "val", 0, 256, False)
        if t == 0:
            rest_v()
            act(A("tab", 2048, TW), A("ones", 0, TW - 2048), F.Identity, bias=128.0 - K, scale=0.0)
            act(A("cab", 2064, TW), A("ones", 0, TW - 2064), F.Identity, scale=0.0)
        ts(A("pl"), P(4, 0, 16), float(16 * m0 + off), O.add)
        ts(A("du"), ind(A("tab"), A("pl")), 1.0 / 256, O.mult, K / 256 - 0.5, O.add)
        act(A("abc"), ind(A("cab"), A("pl")), F.Copy)
        for h in range(2):
            mm(P(7, 128 * h, 128 * h + 128), A("abc", 128 * h, 128 * h + 128), A("idb"))
        for a, b in CH:
            act(A("lg", 16 * a, 16 * b), ind(A("hamb"), A("du", a, b)), F.Copy)
        ts(A("d16"), A("du"), 2048.0, O.subtract)
        cp(A("ct"), P(7, 0, 256))
        if t == 0:
            rest_v2()
        for h in range(2):
            for e in range(2):
                mm(P(4, 16 * e + 8 * h, 16 * e + 8 * h + 8), A("d16", 128 * h, 128 * h + 128), A("w12", 8 * e, 8 * e + 8))

        def rep(b):
            mm(P(b % 4, 0, 512), A("ct", 128 * (b // 4), 128 * (b // 4) + 128), A("rexp", 512 * (b % 4), 512 * (b % 4) + 512))

        for b in range(4):
            rep(b)
        mm(P(7, 0, 256), A("gum"), A("d16"))
        mm(P(7, 256, 512), A("gdm"), A("d16"))
        cp(A("ui"), P(4, 0, 32))
        ts(A("ui2"), A("ui"), 4095, O.bitwise_and)
        tt(A("pi"), A("ui2", 0, 16), A("ui2", 16, 32), O.mult)
        ts(A("h16"), A("pi"), 1, O.arith_shift_right, 0x7FFFFFF0, O.bitwise_and)
        ts(A("h16t"), A("h16"), float(16 * t), O.add)
        cp(A("lg", 3584, 4096), ind(A("hamb"), A("du", 224, 256)))
        for b in range(8):
            s = 512 * b
            tt(A("mn", s, s + 512), A("lg", s, s + 512), P(b % 4, 0, 512), O.min)
            if b < 4:
                rep(b + 4)
            if b % 4 == 3:
                h = b // 4
                for k in range(16):
                    mm(P(6, 128 * h + k, 128 * h + 128, 16), A("mn", 2048 * h + k, 2048 * h + 2048, 16), A("blk592"))
        if t == 0:
            ts(A("rvk", 0, 256), A("rvk", 0, 256), -1.0, O.mult)
            ts(A("trb"), A("trb"), -1.0, O.mult)
        cp(A("ti"), ind(A("tab"), A("pl")))
        ts(A("fi"), A("ti"), 255, O.bitwise_and, 2, O.arith_shift_right)
        ts(A("ff"), A("fi"), 32.0, O.subtract)
        act(P(7, 0, 256), P(7, 0, 256), F.Identity, bias=col(9))
        act(P(7, 256, 512), P(7, 256, 512), F.Identity, bias=col(10))
        mm(P(5, 0, 256), A("idb"), A("d16"))
        scan(A("km"), A("kscan"), P(6, 0, 256), O.add, O.max)
        tt(A("si"), A("km", 15, 256, 16), A("h16t"), O.add)
        ts(A("vk", 0, 16), A("si"), 4, O.arith_shift_right, 4095, O.bitwise_and)
        ts(A("vk", 16, 32), A("si"), 15, O.bitwise_and)
        ts(A("vk16"), A("vk"), 2048.0, O.subtract)
        mm(P(4, 0, 128, 1, 0, 32), A("vk16"), A("idb"))
        cp(A("t32", 0, 128, 1, 0, 32), P(4, 0, 128, 1, 0, 32))
        for h in range(2):
            s = 128 * h
            mm(P(1, s, s + 128), A("rvk", 256 + s, 256 + s + 128, 1, 0, 32), A("t32", 0, 128, 1, 0, 32))
        for h in range(2):
            s = 128 * h
            mm(P(0, s, s + 128), A("idb"), A("d16", s, s + 128), True, False)
            mm(P(0, s, s + 128), A("rvk", s, s + 128, 1, 0, 32), A("t32", 0, 128, 1, 0, 32), False, True)
        ts(A("ma"), P(1, 0, 256), col(7), O.is_ge)
        act(A("sd"), P(0, 0, 256), F.Sign)
        act(A("mb"), P(1, 0, 256), F.Relu, bias=col(8), scale=-8192.0)
        wsum(P(3, 0, 16), "em", "sd", 0, 256)
        tt(P(2, 0, 256), P(7, 0, 256), A("ma"), O.mult)
        tt(A("lo"), P(7, 256, 512), A("mb"), O.min)
        tt(A("t1"), A("lo"), P(0, 0, 256), O.min)
        tt(A("tt"), A("t1"), P(2, 0, 256), O.max)
        tt(A("ch16"), P(5, 0, 256), A("tt"), O.subtract)
        act(A("st_"), A("tt"), F.Sign)
        mm(P(5, 256, 512), A("blk"), A("st_"))
        whash("ch16")
        act(A("fa"), A("abc"), F.Relu, bias=-1.0)
        mm(P(2, 0, 256), A("blk"), A("fa"))
        act(A("fs"), P(2, 0, 256), F.Sign, bias=-0.5)
        cp(A("vo"), P(3, 0, 16))
        ts(A("vo2"), A("vo"), 1, O.bitwise_and)
        tt(A("bad4"), A("vo2"), A("nt"), O.max)
        ts(A("bad4"), A("bad4"), 0.0, O.is_gt, 4.0, O.mult)
        tt(A("bo"), A("bad4"), A("iow4"), O.mult)
        ts(A("chp"), A("ch16"), 256.0, O.mult, 2048.0 * 256 + 128, O.add)
        cp(A("npi"), P(5, 256, 512))
        ts(A("npa"), A("npi"), 1, O.bitwise_and)
        ts(P(1, 0, 256), A("npa"), 2.0, O.mult, -1.0, O.add)
        tt(P(1, 0, 256), P(1, 0, 256), A("ff"), O.mult)
        tt(A("pk"), P(1, 0, 256), A("chp"), O.add)
        mix()
        ts(A("own"), A("pi"), 5, O.arith_shift_right, 3, O.bitwise_and)
        tt(A("own2"), A("own"), A("bad4"), O.max)
        for o in range(4):
            ts(A("oh", 16 * o, 16 * o + 16), A("own2"), float(o), O.is_equal)
        mm(P(7, 64, 128), A("blk"), A("oh"))
        mm(P(4, 0, 64), A("ones", 0, 128, 1, 0, 1), A("orow", 0, 64, 1, 0, 1), True, False)
        mm(P(4, 0, 64), A("trb"), A("oh"), False, True)
        scan(A("inc"), A("m64"), P(7, 64, 128), O.mult, O.add)
        tt(A("rk"), A("inc"), P(4, 0, 64), O.add)
        tt(A("mk"), A("rk"), A("oh"), O.mult)
        mm(P(3, 0, 16), A("idb"), A("bo"), True, False)
        for o in range(4):
            mm(P(3, 0, 16), A("idb"), A("mk", 16 * o, 16 * o + 16), False, o == 3)
        cp(A("sl"), P(3, 0, 16))
        sb, ar, arr = "sb%d" % t, "ar%d" % t, "arr%d" % t
        cp(ind(A(sb), A("sl")), A("pk"))
        trs = []
        for o, es in plan(topo, T.cores, rank):
            rid, pid = topo.addr(T.cores[o])[:2]
            trs.append(RemoteDMATransfer(dst_ids=[DstId(rid=rid, pnc=pid)], dma_engine_mask=sum(1 << e for e in es), remote_sem=T.sem[arr],
                                         src=A(sb, 256 * o, 256 * o + 64)[0], dst=A(ar, 64 * rank, 64 * rank + 64)[0]))
        need("g", [], [A(sb)])
        g.remote_dma_fused(trs, local_sem=T.sem.sent)
        got = sum(len(es) for q in range(N) if q != rank for o, es in plan(topo, T.cores, q) if o == rank)
        if t == 0:
            sel(A("bc"), one(2048), [[-1, 16], [-16, 8], [0, 16]], O.is_equal, 0.0, 0, 1)
            iota(A("mc"), [[2048, 8], [0, 16]], 0, 0)
            iota(A("xio"), [[1, 16]], 0, 0)
        if not last:
            round_g(t + 1)
        cp(A(ar, 64 * rank, 64 * rank + 64), A(sb, 256 * rank, 256 * rank + 64))
        ts(A("ci"), A("ti"), 255, O.bitwise_and)
        ts(A("cc"), A("ci"), 128.0, O.subtract)
        act(A("sgc"), A("cc"), F.Sign)
        if t == 0:
            for c in range(4):
                s = 512 * c
                mm(P(c % 3, 0, 512), A("blk"), A("cab", s, s + 512))
                act(P(c % 3, 0, 512), P(c % 3, 0, 512), F.Sign, bias=-0.5)
                tt(A("tab", s, s + 512), A("tab", s, s + 512), P(c % 3, 0, 512), O.mult)
        if not last:
            cp(ind(A("cab"), A("pl")), A("fa"))
        tt(A("fg"), A("ti"), A("sgc"), O.subtract)
        tt(A("ft"), A("fg"), A("fs"), O.mult)
        cp(ind(A("tab"), A("pl")), A("ft"))
        if not last:
            iota(A("tab", 2048, DUMP), [[0, DUMP - 2048]], 128 - K, 0)
        ts(A("ai"), A(ar), 8, O.arith_shift_right, extra=[(arr, got)])
        ts(A("a16"), A("ai"), 2048.0, O.subtract)
        whash("a16")
        ts(A("aa"), A("ai"), 256.0, O.mult, 128.0 - K, O.add)
        ts(A("aam"), A("aa"), 256.0, O.subtract)
        ts(A("ac"), A(ar), 255, O.bitwise_and)
        mix(True)
        ts(A("z", 0, 16), A("pi"), 7, O.arith_shift_right, 2047, O.bitwise_and)
        tt(A("z", 16, 32), A("z", 0, 16), A("st1"), O.add)
        ts(A("zi2", 0, 32), A("z", 0, 32), 2047, O.bitwise_and)
        cp(A("zu", 0, 32), A("zi2", 0, 32))
        late = []
        for m in range(8):
            s = 256 * m
            tt(A("df", s, s + 256), ind(A("tab"), A("zu", 16 * m, 16 * m + 16)), A("aa"), O.subtract)
            if m == 0:
                tt(A("z", 32, 64), A("z", 0, 32), A("st2"), O.add)
                tt(A("z", 64, 128), A("z", 0, 64), A("st4"), O.add)
                ts(A("zi2", 32, 128), A("z", 32, 128), 2047, O.bitwise_and)
                cp(A("zu", 32, 128), A("zi2", 32, 128))
            act(A("ab", s, s + 256), A("df", s, s + 256), F.Abs)
            while late:
                z = late.pop()
                ts(A("rl", z, z + 256), A("ab", z, z + 256), 127.0, O.subtract, 0.0, O.max)
            if m % 2 == 0:
                late.append(s)
            else:
                act(A("rl", s, s + 256), A("ab", s, s + 256), F.Relu, bias=-127.0)
            if m % 4 == 3:
                wsum(P(m // 4, 0, 64), "em", "rl", 256 * m - 768, 256 * m + 256)
        tt(A("mz"), A("mc"), A("zi2"), O.add)
        if t == 0:
            ts(A("tm"), A("xio"), col(0), O.is_le, 0.5, O.mult)
        if not last:
            round_v(t + 1)
        for h in range(2):
            a, b = 64 * h, 64 * h + 64
            ts(A("k1", a, b), P(h, 0, 64), 0.5, O.is_gt, 32768.0, O.mult)
            ts(A("k2", a, b), P(h, 0, 64), 8.4e7, O.is_gt, -16384.0, O.mult)
            tt(A("k1", a, b), A("k1", a, b), A("mz", a, b), O.add)
            tt(A("k3", a, b), A("k1", a, b), A("k2", a, b), O.add)
        tt(A("k4"), A("k3", 0, 64), A("k3", 64, 128), O.min)
        tt(A("k5"), A("k4", 0, 32), A("k4", 32, 64), O.min)
        tt(A("kmi"), A("k5", 0, 16), A("k5", 16, 32), O.min)
        ts(A("inv"), A("kmi"), 32768.0, O.is_ge, -4096.0, O.mult)
        ts(A("plc"), A("kmi"), 2047, O.bitwise_and)
        tt(A("key16"), A("plc"), A("inv"), O.add)
        tt(A("keyw"), A("plc"), A("inv"), O.add)
        cp(A("plu"), A("plc"))
        mm(P(3, 0, 256), A("blk"), A("zb"), True, False)
        for r in range(16):
            mm(P(2, r, 256, 16), A("bc", 128 * r, 128 * r + 128), A("key16"))
        cp(A("oi"), ind(A("tab"), A("plu")))
        ts(A("oc"), A("oi"), 255, O.bitwise_and)
        for x in range(16):
            act(A("kr", x, 256, 16), A("keyw"), F.Identity, bias=A("tm", x, x + 1))
        cp(A("kb16"), P(2, 0, 256))
        for c in range(15):
            e = A("eq", 256 * c + 16 * c + 16, 256 * c + 256)
            ts(e, A("kb16", 16 * c + 16, 256), A("keyw", c, c + 1), O.is_equal)
            mm(P(3, 16 * c + 16, 256), A("blk"), e, False, False)
            if c == 13:
                tt(A("dm"), P(2, 0, 256), A("kr"), O.is_equal)
        mm(P(3, 0, 256), A("blk"), A("dm"), False, True)
        act(A("lsb"), P(3, 0, 256), F.Copy)
        tt(A("cs"), A("oc"), A("ac"), O.add)
        ts(A("cn"), A("cs"), 129.0, O.max, 383.0, O.min)
        act(A("ent"), A("cn"), F.Abs, bias=-256.0)
        wsum(P(4, 0, 16), "em", "lsb", 0, 256)
        tt(A("tg"), A("aam"), A("cn"), O.add)
        mm(P(5, 0, 256), A("blk"), A("ent"))
        act(A("es"), P(5, 0, 256), F.Sign, bias=-0.5)
        tt(A("ls"), A("inv"), P(4, 0, 16), O.subtract)
        ts(A("ls2"), A("ls"), -0.5, O.is_lt)
        tt(A("ls"), A("ls2"), A("dumpc"), O.mult)
        tt(A("fo"), A("ls"), A("plc"), O.max)
        cp(A("fou"), A("fo"))
        if not last:
            cp(ind(A("cab"), A("fou")), A("ent"))
            cp(A("cab", 2048, 2064), A("cab", 0, 16))
        tt(A("tn"), A("tg"), A("es"), O.mult)
        cp(ind(A("tab"), A("fou")), A("tn"))

    for c in range(4):
        s = 512 * c
        act(A("ab", s, s + 512), A("tab", s, s + 512), F.Abs)
        ts(A("df", s, s + 512), A("ab", s, s + 512), -1.0, O.mult, float(K), O.add)
        store("y", "out%d" % c, T.y[:, s:s + 512], A("df", s, s + 512))
    for c in range(4):
        g.wait_ge(T.sem["out%d" % c], 16)
    g.wait_ge(T.sem.ldh, 16)
    g.wait_ge(T.sem.sent, 8 * RO)
    for q in ("v", "s", "t", "g"):
        g.wait_ge(T.sem[SEMOF[q]], count[q])
